import numpy as np
import ml_dtypes


def mxq(x, axis, fmt="e4m3"):
    dtype, down = {"e4m3": (ml_dtypes.float8_e4m3fn, 7), "e5m2": (ml_dtypes.float8_e5m2, 14)}[fmt]
    v = np.moveaxis(np.asarray(x, np.float32).astype(ml_dtypes.bfloat16).astype(np.float64), axis, -1)
    blocks = v.reshape(v.shape[:-1] + (-1, 32))
    amax = np.abs(blocks).max(-1, keepdims=True)
    byte = np.maximum(np.where(amax > 0, np.frexp(amax)[1] - 1 + 127, 0) - down, 1)
    scale = np.exp2(byte - 127.0)
    codes = (blocks / scale).astype(np.float32).astype(dtype).astype(np.float64)
    return np.moveaxis((codes * scale).reshape(v.shape), -1, axis)


WIDE = False


def mx_kscale(k):
    if not WIDE:
        return np.ones(k)
    levels = np.array([10, -10, 5, -5, 0])
    if k % 512:
        return np.exp2(np.random.permutation(np.resize(levels, k // 32))).repeat(32)
    a = np.empty((k // 512, 16))
    for p in range(k // 512):
        a[p, :8] = np.random.permutation(np.resize(levels, 8))
        for g in range(8):
            far = levels[np.abs(levels - a[p, g]) >= 10]
            a[p, g + 8] = far[np.random.randint(len(far))]
    return np.exp2(a.ravel()).repeat(32)


def f64(x):
    return np.asarray(x).astype(np.float64)


def striped(idx):
    return np.tile(idx.reshape(-1, 16).T, (8, 1)).astype(np.uint16)


def unstriped(offs):
    return offs[:16].T.reshape(-1).astype(np.int64)


E2M1 = np.array([0.0, 0.5, 1.0, 1.5, 2.0, 3.0, 4.0, 6.0, -0.0, -0.5, -1.0, -1.5, -2.0, -3.0, -4.0, -6.0])


def pack_weight(w, fmt):
    k, n = w.shape
    w = f64(np.asarray(w, np.float32).astype(ml_dtypes.bfloat16)).reshape(k // 32, 32, n)
    amax = np.abs(w).max(1)
    if fmt == "e4m3":
        byte = np.frexp(amax)[1] - 1 + 127 - 7
    else:
        mant, ex = np.frexp(amax / 6.0)
        byte = np.where(mant > 0.5, ex, ex - 1) + 127
    byte = np.clip(np.where(amax > 0, byte, 1), 1, 254)
    scaled = (w * np.exp2(127.0 - byte)[:, None, :]).reshape(k, n).astype(np.float32)
    by_word = np.ascontiguousarray(scaled.reshape(k // 512, 128, 4, n).transpose(0, 1, 3, 2))
    if fmt == "e4m3":
        words = by_word.astype(ml_dtypes.float8_e4m3fn).view(np.uint8)
    else:
        c = by_word.astype(ml_dtypes.float4_e2m1fn).view(np.uint8) & 0xF
        words = (c[..., 0::2] | (c[..., 1::2] << 4)).reshape(k // 512, 128, 2 * n)
    return np.ascontiguousarray(words), np.ascontiguousarray(byte.astype(np.uint8).reshape(k // 512, 16, n))


def unpack_weight(words, scales, fmt):
    g, _, n = scales.shape
    words = np.ascontiguousarray(words).reshape(g, 128, n, -1)
    if fmt == "e4m3":
        vals = words.view(ml_dtypes.float8_e4m3fn).astype(np.float64)
    else:
        nib = np.empty((g, 128, n, 4), np.uint8)
        nib[..., 0::2] = words & 0xF
        nib[..., 1::2] = words >> 4
        vals = E2M1[nib]
    vals = vals * np.repeat(np.exp2(scales.astype(np.float64) - 127.0), 8, axis=1)[..., None]
    return vals.transpose(0, 1, 3, 2).reshape(g * 512, n)


def relu(v):
    return np.maximum(v, 0.0)


K, T, E, C, H, N = 2048, 1024, 4, 256, 512, 512


def by_expert(wq, xq):
    return np.concatenate([wq[e].T @ xq[:, e * C:(e + 1) * C] for e in range(E)], axis=1)


def setup_inputs():
    n = np.random.standard_normal
    s = mx_kscale(K)
    u = mx_kscale(H)
    slot_token = np.random.permutation(T)[:E * C]
    x = pack_weight(n((K, T)) * s[:, None], "e4m3")
    w1 = [pack_weight(m, "e4m3") for m in n((E, K, H)) / np.sqrt(K) / s[None, :, None] * u]
    w2 = pack_weight(n((H, N)) / np.sqrt(H) / u[:, None], "e2m1")
    return {
        "x_words": x[0],
        "x_scales": x[1],
        "w1_words": np.stack([m[0] for m in w1]),
        "w1_scales": np.stack([m[1] for m in w1]),
        "w2_words": w2[0],
        "w2_scales": w2[1],
        "gate": np.tile(np.random.uniform(0.2, 1.0, E * C), (128, 1)).astype(np.float32),
        "offs": striped(slot_token),
    }


def reference(x_words, x_scales, w1_words, w1_scales, w2_words, w2_scales, gate, offs):
    w1 = np.stack([unpack_weight(w1_words[e], w1_scales[e], "e4m3") for e in range(E)])
    w2 = unpack_weight(w2_words, w2_scales, "e2m1")
    idx = unstriped(offs)
    xq = unpack_weight(x_words, x_scales, "e4m3")[:, idx]
    h = relu(by_expert(w1, xq))
    c = np.zeros((H, T))
    c[:, idx] = f64(gate[:1]) * h
    return w2.T @ mxq(c, 0, "e4m3")

@@ -1,0 +1,176 @@
+from contextlib import ExitStack
+
+import concourse.mybir as mybir
+from concourse.masks import make_identity
+
+K, T, E, C, H, N = 2048, 1024, 4, 256, 512, 512
+FLOPS = 2 * K * H * E * C + 2 * H * N * T
+
+F32 = mybir.dt.float32
+BF16 = mybir.dt.bfloat16
+I32 = mybir.dt.int32
+U32 = mybir.dt.uint32
+U16 = mybir.dt.uint16
+U8 = mybir.dt.uint8
+FP8X4 = mybir.dt.float8_e4m3fn_x4
+FP4X4 = mybir.dt.float4_e2m1fn_x4
+ACT = mybir.ActivationFunctionType
+
+P = 128
+PASSES = K // 512
+HALF = E * C // 2
+CHUNKS = [(0, 256), (256, 256), (512, 512)]
+
+
+def tile_moe_sdn_lin_relu_kernel(tc, x_words, x_scales, w1_words, w1_scales, w2_words, w2_scales, gate, offs, out):
+    nc = tc.nc
+    with ExitStack() as ctx:
+        keep = ctx.enter_context(tc.tile_pool(name="keep", bufs=1))
+        ring = ctx.enter_context(tc.tile_pool(name="ring", bufs=3))
+        banks = ctx.enter_context(tc.psum_pool(name="banks", bufs=5))
+        turned = ctx.enter_context(tc.psum_pool(name="turned", bufs=3))
+
+        offsets = keep.tile([P, E * C // 16], U16, name="offsets")
+        nc.sync.dma_start(offsets[:], offs)
+
+        x_plane = keep.tile([P, T], U8, name="x_plane", align_bytes=64)
+        w1_plane = keep.tile([P, E, H], U8, name="w1_plane", align_bytes=64)
+        w2_plane = keep.tile([P, N], U8, name="w2_plane", align_bytes=64)
+        nc.vector.memset(x_plane[:].bitcast(I32), 0)
+        nc.vector.memset(w1_plane[:].rearrange("p e h -> p (e h)").bitcast(I32), 0)
+        nc.vector.memset(w2_plane[:].bitcast(I32), 0)
+
+        gate_rows = keep.tile([P, P], F32, name="gate_rows")
+        ident = keep.tile([P, P], F32, name="ident")
+        nc.gpsimd.memset(gate_rows[:], 0.0)
+        make_identity(nc, ident[:])
+        nc.scalar.dma_start(gate_rows[0:8, :], gate[0, :].rearrange("(c p) -> c p", p=P))
+
+        for q in range(4):
+            nc.sync.dma_start(x_plane[32 * q : 32 * q + 16, :].bitcast(I32), x_scales[:, 4 * q : 4 * q + 4, :].bitcast(I32))
+        x_tok = []
+        for s in range(PASSES):
+            t_ = keep.tile([P, T], I32, name=f"x_tok{s}", align_bytes=64)
+            nc.sync.dma_start(t_[:], x_words[s].rearrange("p t d -> p (t d)").bitcast(I32))
+            x_tok.append(t_)
+
+        w1 = {}
+        for e in range(E):
+            for q in range(4):
+                nc.sync.dma_start(w1_plane[32 * q : 32 * q + 16, e, :].bitcast(I32), w1_scales[e, :, 4 * q : 4 * q + 4, :].bitcast(I32))
+            step = 1 if e == E - 1 else 2
+            for s0 in range(0, PASSES, step):
+                t_ = keep.tile([P, step, H], I32, name=f"w1_{e}_{s0}", align_bytes=64)
+                nc.sync.dma_start(t_[:], w1_words[e, s0 : s0 + step].rearrange("s p i d -> p s (i d)").bitcast(I32))
+                for s in range(s0, s0 + step):
+                    w1[e, s] = t_[:, s - s0, :]
+        w2 = keep.tile([P, 2 * N], U8, name="w2", align_bytes=64)
+        nc.sync.dma_start(w2[:].bitcast(I32), w2_words[0].bitcast(I32))
+        for q in range(4):
+            nc.sync.dma_start(w2_plane[32 * q : 32 * q + 4, :].bitcast(I32), w2_scales[0, 4 * q : 4 * q + 4, :].bitcast(I32))
+
+        gate_ps = turned.tile([P, 4, P], F32, name="turn")
+        nc.tensor.transpose(gate_ps[:, 0, :], gate_rows[:], ident[:])
+        gate_col = keep.tile([P, 8], F32, name="gate_col")
+        nc.scalar.copy(gate_col[:], gate_ps[:, 0, 0:8])
+
+        slot_words = {}
+        slot_plane = []
+        for half in range(2):
+            cols = offsets[:, half * HALF // 16 : (half + 1) * HALF // 16]
+            plane = keep.tile([P, HALF], U8, name=f"slot_plane{half}", align_bytes=64)
+            nc.vector.tensor_copy(plane[:], x_plane[:].indirect(cols))
+            slot_plane.append(plane)
+            for s in range(PASSES):
+                t_ = keep.tile([P, HALF], U32, name=f"slot_words{half}_{s}", align_bytes=64)
+                nc.vector.tensor_copy(t_[:], x_tok[s][:].bitcast(U32).indirect(cols))
+                slot_words[half, s] = t_
+
+        by_slot = keep.tile([P, 4, E * C], F32, name="by_slot")
+        by_token = [keep.tile([P, 2 * T], F32, name=f"by_token{d}") for d in range(4)]
+
+        for e in range(E):
+            half, c0 = divmod(e * C, HALF)
+            acc = [banks.tile([P, H], F32, name="bank") for j in range(2)]
+            for s in range(PASSES):
+                for j in range(2):
+                    slots = slice(c0 + j * P, c0 + (j + 1) * P)
+                    nc.tensor.matmul_mx(
+                        out=acc[j][:],
+                        lhsT=slot_words[half, s][:, slots].bitcast(FP8X4),
+                        lhsT_scale=slot_plane[half][4 * s :, slots],
+                        rhs=w1[e, s].bitcast(FP8X4),
+                        rhs_scale=w1_plane[4 * s :, e, :],
+                        start=(s == 0),
+                        stop=(s == PASSES - 1),
+                    )
+            for j in range(2):
+                pos = ring.tile([P, 4, P], F32, name="pos")
+                nc.scalar.activation(pos[:], acc[j][:].rearrange("s (p d) -> s d p", d=4), ACT.Relu)
+                gated = ring.tile([P, 4, P], F32, name="gated")
+                nc.scalar.activation(gated[:], pos[:], ACT.Copy, scale=gate_col[:, 2 * e + j : 2 * e + j + 1])
+                turn = turned.tile([P, 4, P], F32, name="turn")
+                for d in range(4):
+                    nc.tensor.transpose(turn[:, d, :], gated[:, d, :], ident[:])
+                nc.scalar.copy(by_slot[:, :, e * C + j * P : e * C + (j + 1) * P], turn[:])
+
+        def scatter(d, s0, s1):
+            nc.vector.tensor_copy(by_token[d][:].indirect(offsets[:, s0 // 16 : s1 // 16]), by_slot[:, d, s0:s1])
+
+        grouped = [keep.tile([P, width, 4], BF16, name=f"grouped{n}", align_bytes=64) for n, (t0, width) in enumerate(CHUNKS)]
+        scatter(3, 0, HALF)
+        scatter(0, 0, HALF)
+        scatter(1, 0, HALF)
+        scatter(3, HALF, 2 * HALF)
+        nc.scalar.copy(by_token[2][:, T : 2 * T], by_token[3][:, 0:T])
+        scatter(0, HALF, 2 * HALF)
+        scatter(1, HALF, 2 * HALF)
+        for d in range(2):
+            for n, (t0, width) in enumerate(CHUNKS):
+                nc.scalar.copy(grouped[n][:, :, d], by_token[d][:, t0 : t0 + width])
+        scatter(2, 0, 2 * HALF)
+        upper = by_token[2][:].rearrange("p (u t) -> p t u", u=2)
+        codes, scales = [], []
+
+        def interleave(n):
+            t0, width = CHUNKS[n]
+            nc.vector.tensor_copy(grouped[n][:, :, 2:4], upper[:, t0 : t0 + width, :])
+
+        def quantise(n):
+            width = CHUNKS[n][1]
+            c_ = keep.tile([P, width], U32, name=f"codes{n}", align_bytes=64)
+            s_ = keep.tile([P, width], U8, name=f"scales{n}", align_bytes=64)
+            nc.vector.quantize_mx(out=c_[:].bitcast(FP8X4), scales=s_[:], in_=grouped[n][:].rearrange("p t d -> p (t d)"))
+            codes.append(c_)
+            scales.append(s_)
+
+        interleave(0)
+        interleave(1)
+        quantise(0)
+        interleave(2)
+        quantise(1)
+        quantise(2)
+
+        rows = out.rearrange("(m p) t -> p m t", p=P)
+        count = 0
+        for n, (t0, width) in enumerate(CHUNKS):
+            per_bank = 512 // width
+            for m0 in range(0, N // P, per_bank):
+                bank = banks.tile([P, H], F32, name="bank")
+                for m in range(m0, m0 + per_bank):
+                    nc.tensor.matmul_mx(
+                        out=bank[:, (m - m0) * width : (m - m0 + 1) * width],
+                        lhsT=w2[:, 2 * m * P : 2 * (m + 1) * P].bitcast(FP4X4),
+                        lhsT_scale=w2_plane[:, m * P : (m + 1) * P],
+                        rhs=codes[n][:].bitcast(FP8X4),
+                        rhs_scale=scales[n][:],
+                        start=True,
+                        stop=True,
+                    )
+                res = keep.tile([P, H], F32, name=f"res{count}")
+                if count in (5, 7):
+                    nc.vector.tensor_copy(res[:], bank[:])
+                else:
+                    nc.scalar.copy(res[:], bank[:])
+                nc.sync.dma_start(rows[:, m0 : m0 + per_bank, t0 : t0 + width], res[:].rearrange("p (m t) -> p m t", m=per_bank))
+                count += 1

@@ -14,19 +14,20 @@ U16 = mybir.dt.uint16
 U8 = mybir.dt.uint8
 FP8X4 = mybir.dt.float8_e4m3fn_x4
 FP4X4 = mybir.dt.float4_e2m1fn_x4
+MULT = mybir.AluOpType.mult
 ACT = mybir.ActivationFunctionType
 
 P = 128
 PASSES = K // 512
 HALF = E * C // 2
-CHUNKS = [(0, 256), (256, 256), (512, 512)]
+CHUNKS = [(0, 128, 2), (128, 128, 4), (256, 256, 2), (512, 512, 1)]
 
 
 def tile_moe_sdn_lin_relu_kernel(tc, x_words, x_scales, w1_words, w1_scales, w2_words, w2_scales, gate, offs, out):
     nc = tc.nc
     with ExitStack() as ctx:
         keep = ctx.enter_context(tc.tile_pool(name="keep", bufs=1))
-        ring = ctx.enter_context(tc.tile_pool(name="ring", bufs=3))
+        ring = ctx.enter_context(tc.tile_pool(name="ring", bufs=4))
         banks = ctx.enter_context(tc.psum_pool(name="banks", bufs=5))
         turned = ctx.enter_context(tc.psum_pool(name="turned", bufs=3))
 
@@ -34,60 +35,84 @@ def tile_moe_sdn_lin_relu_kernel(tc, x_words, x_scales, w1_words, w1_scales, w2_
         nc.sync.dma_start(offsets[:], offs)
 
         x_plane = keep.tile([P, T], U8, name="x_plane", align_bytes=64)
-        w1_plane = keep.tile([P, E, H], U8, name="w1_plane", align_bytes=64)
+        w1_plane = [keep.tile([P, H], U8, name=f"w1_plane{e}", align_bytes=64) for e in range(E)]
         w2_plane = keep.tile([P, N], U8, name="w2_plane", align_bytes=64)
-        nc.vector.memset(x_plane[:].bitcast(I32), 0)
-        nc.vector.memset(w1_plane[:].rearrange("p e h -> p (e h)").bitcast(I32), 0)
+        nc.gpsimd.memset(x_plane[:].bitcast(I32), 0)
+        nc.gpsimd.memset(w1_plane[0][:].bitcast(I32), 0)
+        for e in range(1, E):
+            nc.vector.memset(w1_plane[e][:].bitcast(I32), 0)
         nc.vector.memset(w2_plane[:].bitcast(I32), 0)
 
-        gate_rows = keep.tile([P, P], F32, name="gate_rows")
         ident = keep.tile([P, P], F32, name="ident")
-        nc.gpsimd.memset(gate_rows[:], 0.0)
         make_identity(nc, ident[:])
-        nc.scalar.dma_start(gate_rows[0:8, :], gate[0, :].rearrange("(c p) -> c p", p=P))
+
+        x_tok, w1 = {}, {}
+
+        def load_tokens(s):
+            t_ = keep.tile([P, T], I32, name=f"x_tok{s}", align_bytes=64)
+            nc.sync.dma_start(t_[:], x_words[s].rearrange("p t d -> p (t d)").bitcast(I32))
+            x_tok[s] = t_
+
+        def load_w1_scales(e):
+            for q in range(4):
+                nc.sync.dma_start(w1_plane[e][32 * q : 32 * q + 16, :].bitcast(I32), w1_scales[e, :, 4 * q : 4 * q + 4, :].bitcast(I32))
+
+        def load_w1(e, s0):
+            t_ = keep.tile([P, 2, H], I32, name=f"w1_{e}_{s0}", align_bytes=64)
+            nc.sync.dma_start(t_[:], w1_words[e, s0 : s0 + 2].rearrange("s p i d -> p s (i d)").bitcast(I32))
+            for s in range(2):
+                w1[e, s0 + s] = t_[:, s, :]
+
+        gates = []
+
+        def load_gate(half):
+            t_ = keep.tile([P, HALF], F32, name=f"gate{half}")
+            nc.sync.dma_start(t_[:], gate[:, half * HALF : (half + 1) * HALF])
+            gates.append(t_)
 
         for q in range(4):
             nc.sync.dma_start(x_plane[32 * q : 32 * q + 16, :].bitcast(I32), x_scales[:, 4 * q : 4 * q + 4, :].bitcast(I32))
-        x_tok = []
-        for s in range(PASSES):
-            t_ = keep.tile([P, T], I32, name=f"x_tok{s}", align_bytes=64)
-            nc.sync.dma_start(t_[:], x_words[s].rearrange("p t d -> p (t d)").bitcast(I32))
-            x_tok.append(t_)
-
-        w1 = {}
-        for e in range(E):
-            for q in range(4):
-                nc.sync.dma_start(w1_plane[32 * q : 32 * q + 16, e, :].bitcast(I32), w1_scales[e, :, 4 * q : 4 * q + 4, :].bitcast(I32))
-            step = 1 if e == E - 1 else 2
-            for s0 in range(0, PASSES, step):
-                t_ = keep.tile([P, step, H], I32, name=f"w1_{e}_{s0}", align_bytes=64)
-                nc.sync.dma_start(t_[:], w1_words[e, s0 : s0 + step].rearrange("s p i d -> p s (i d)").bitcast(I32))
-                for s in range(s0, s0 + step):
-                    w1[e, s] = t_[:, s - s0, :]
+        load_tokens(0)
+        load_tokens(1)
+        load_w1_scales(0)
+        load_w1(0, 0)
+        load_tokens(2)
+        load_tokens(3)
+        load_w1(0, 2)
+        for e in range(1, E):
+            load_w1_scales(e)
+            load_w1(e, 0)
+            load_w1(e, 2)
+            if e % 2 == 1:
+                load_gate(e // 2)
         w2 = keep.tile([P, 2 * N], U8, name="w2", align_bytes=64)
         nc.sync.dma_start(w2[:].bitcast(I32), w2_words[0].bitcast(I32))
         for q in range(4):
             nc.sync.dma_start(w2_plane[32 * q : 32 * q + 4, :].bitcast(I32), w2_scales[0, 4 * q : 4 * q + 4, :].bitcast(I32))
 
-        gate_ps = turned.tile([P, 4, P], F32, name="turn")
-        nc.tensor.transpose(gate_ps[:, 0, :], gate_rows[:], ident[:])
-        gate_col = keep.tile([P, 8], F32, name="gate_col")
-        nc.scalar.copy(gate_col[:], gate_ps[:, 0, 0:8])
+        slot_words, slot_plane = {}, {}
 
-        slot_words = {}
-        slot_plane = []
-        for half in range(2):
-            cols = offsets[:, half * HALF // 16 : (half + 1) * HALF // 16]
+        def gather_scales(half):
             plane = keep.tile([P, HALF], U8, name=f"slot_plane{half}", align_bytes=64)
-            nc.vector.tensor_copy(plane[:], x_plane[:].indirect(cols))
-            slot_plane.append(plane)
-            for s in range(PASSES):
-                t_ = keep.tile([P, HALF], U32, name=f"slot_words{half}_{s}", align_bytes=64)
-                nc.vector.tensor_copy(t_[:], x_tok[s][:].bitcast(U32).indirect(cols))
-                slot_words[half, s] = t_
+            nc.vector.tensor_copy(plane[:], x_plane[:].indirect(offsets[:, half * HALF // 16 : (half + 1) * HALF // 16]))
+            slot_plane[half] = plane
 
-        by_slot = keep.tile([P, 4, E * C], F32, name="by_slot")
-        by_token = [keep.tile([P, 2 * T], F32, name=f"by_token{d}") for d in range(4)]
+        def gather_words(half, s):
+            t_ = keep.tile([P, HALF], U32, name=f"slot_words{half}_{s}", align_bytes=64)
+            nc.vector.tensor_copy(t_[:], x_tok[s][:].bitcast(U32).indirect(offsets[:, half * HALF // 16 : (half + 1) * HALF // 16]))
+            slot_words[half, s] = t_
+
+        gather_scales(0)
+        gather_words(0, 0)
+        gather_words(0, 1)
+        gather_scales(1)
+        gather_words(0, 2)
+        gather_words(0, 3)
+        for s in range(PASSES):
+            gather_words(1, s)
+
+        by_slot = [keep.tile([P, 4, HALF], F32, name=f"by_slot{half}") for half in range(2)]
+        by_token = [keep.tile([P, 2 * T if d == 2 else T], F32, name=f"by_token{d}") for d in range(4)]
 
         for e in range(E):
             half, c0 = divmod(e * C, HALF)
@@ -100,40 +125,41 @@ def tile_moe_sdn_lin_relu_kernel(tc, x_words, x_scales, w1_words, w1_scales, w2_
                         lhsT=slot_words[half, s][:, slots].bitcast(FP8X4),
                         lhsT_scale=slot_plane[half][4 * s :, slots],
                         rhs=w1[e, s].bitcast(FP8X4),
-                        rhs_scale=w1_plane[4 * s :, e, :],
+                        rhs_scale=w1_plane[e][4 * s :, :],
                         start=(s == 0),
                         stop=(s == PASSES - 1),
                     )
+            pos, turn = [], []
             for j in range(2):
-                pos = ring.tile([P, 4, P], F32, name="pos")
-                nc.scalar.activation(pos[:], acc[j][:].rearrange("s (p d) -> s d p", d=4), ACT.Relu)
-                gated = ring.tile([P, 4, P], F32, name="gated")
-                nc.scalar.activation(gated[:], pos[:], ACT.Copy, scale=gate_col[:, 2 * e + j : 2 * e + j + 1])
-                turn = turned.tile([P, 4, P], F32, name="turn")
+                pos.append(ring.tile([P, 4, P], F32, name="pos"))
+                nc.scalar.activation(pos[j][:], acc[j][:].rearrange("s (p d) -> s d p", d=4), ACT.Relu)
+            for j in range(2):
+                turn.append(turned.tile([P, 4, P], F32, name="turn"))
                 for d in range(4):
-                    nc.tensor.transpose(turn[:, d, :], gated[:, d, :], ident[:])
-                nc.scalar.copy(by_slot[:, :, e * C + j * P : e * C + (j + 1) * P], turn[:])
+                    nc.tensor.transpose(turn[j][:, d, :], pos[j][:, d, :], ident[:])
+            for j in range(2):
+                nc.scalar.copy(by_slot[half][:, :, c0 + j * P : c0 + (j + 1) * P], turn[j][:])
 
-        def scatter(d, s0, s1):
-            nc.vector.tensor_copy(by_token[d][:].indirect(offsets[:, s0 // 16 : s1 // 16]), by_slot[:, d, s0:s1])
+        def scatter(d, half, c0, c1):
+            cols = offsets[:, (half * HALF + c0) // 16 : (half * HALF + c1) // 16]
+            nc.vector.tensor_tensor(by_token[d][:].indirect(cols), by_slot[half][:, d, c0:c1], gates[half][:, c0:c1], MULT)
 
-        grouped = [keep.tile([P, width, 4], BF16, name=f"grouped{n}", align_bytes=64) for n, (t0, width) in enumerate(CHUNKS)]
-        scatter(3, 0, HALF)
-        scatter(0, 0, HALF)
-        scatter(1, 0, HALF)
-        scatter(3, HALF, 2 * HALF)
-        nc.scalar.copy(by_token[2][:, T : 2 * T], by_token[3][:, 0:T])
-        scatter(0, HALF, 2 * HALF)
-        scatter(1, HALF, 2 * HALF)
+        grouped = [keep.tile([P, width, 4], BF16, name=f"grouped{n}", align_bytes=64) for n, (t0, width, per_bank) in enumerate(CHUNKS)]
+        for c0 in (0, C):
+            for d in range(4):
+                scatter(d, 0, c0, c0 + C)
+        scatter(3, 1, 0, HALF)
+        nc.scalar.copy(by_token[2][:, T : 2 * T], by_token[3][:])
         for d in range(2):
-            for n, (t0, width) in enumerate(CHUNKS):
+            scatter(d, 1, 0, HALF)
+            for n, (t0, width, per_bank) in enumerate(CHUNKS):
                 nc.scalar.copy(grouped[n][:, :, d], by_token[d][:, t0 : t0 + width])
-        scatter(2, 0, 2 * HALF)
+        scatter(2, 1, 0, HALF)
         upper = by_token[2][:].rearrange("p (u t) -> p t u", u=2)
         codes, scales = [], []
 
         def interleave(n):
-            t0, width = CHUNKS[n]
+            t0, width, per_bank = CHUNKS[n]
             nc.vector.tensor_copy(grouped[n][:, :, 2:4], upper[:, t0 : t0 + width, :])
 
         def quantise(n):
@@ -150,11 +176,12 @@ def tile_moe_sdn_lin_relu_kernel(tc, x_words, x_scales, w1_words, w1_scales, w2_
         interleave(2)
         quantise(1)
         quantise(2)
+        interleave(3)
+        quantise(3)
 
         rows = out.rearrange("(m p) t -> p m t", p=P)
         count = 0
-        for n, (t0, width) in enumerate(CHUNKS):
-            per_bank = 512 // width
+        for n, (t0, width, per_bank) in enumerate(CHUNKS):
             for m0 in range(0, N // P, per_bank):
                 bank = banks.tile([P, H], F32, name="bank")
                 for m in range(m0, m0 + per_bank):
@@ -167,10 +194,10 @@ def tile_moe_sdn_lin_relu_kernel(tc, x_words, x_scales, w1_words, w1_scales, w2_
                         start=True,
                         stop=True,
                     )
-                res = keep.tile([P, H], F32, name=f"res{count}")
-                if count in (5, 7):
-                    nc.vector.tensor_copy(res[:], bank[:])
+                res = keep.tile([P, per_bank * width], F32, name=f"res{count}")
+                if count in (4, 6, 8):
+                    nc.vector.tensor_copy(res[:], bank[:, 0 : per_bank * width])
                 else:
-                    nc.scalar.copy(res[:], bank[:])
+                    nc.scalar.copy(res[:], bank[:, 0 : per_bank * width])
                 nc.sync.dma_start(rows[:, m0 : m0 + per_bank, t0 : t0 + width], res[:].rearrange("p (m t) -> p m t", m=per_bank))
                 count += 1

@@ -37,12 +37,11 @@ def tile_moe_sdn_lin_relu_kernel(tc, x_words, x_scales, w1_words, w1_scales, w2_
         x_plane = keep.tile([P, T], U8, name="x_plane", align_bytes=64)
         w1_plane = [keep.tile([P, H], U8, name=f"w1_plane{e}", align_bytes=64) for e in range(E)]
         w2_plane = keep.tile([P, N], U8, name="w2_plane", align_bytes=64)
-        nc.gpsimd.memset(x_plane[:].bitcast(I32), 0)
+        nc.vector.memset(x_plane[:].bitcast(I32), 0)
         nc.gpsimd.memset(w1_plane[0][:].bitcast(I32), 0)
         for e in range(1, E):
             nc.vector.memset(w1_plane[e][:].bitcast(I32), 0)
         nc.vector.memset(w2_plane[:].bitcast(I32), 0)
-
         ident = keep.tile([P, P], F32, name="ident")
         make_identity(nc, ident[:])
 
@@ -57,10 +56,10 @@ def tile_moe_sdn_lin_relu_kernel(tc, x_words, x_scales, w1_words, w1_scales, w2_
             for q in range(4):
                 nc.sync.dma_start(w1_plane[e][32 * q : 32 * q + 16, :].bitcast(I32), w1_scales[e, :, 4 * q : 4 * q + 4, :].bitcast(I32))
 
-        def load_w1(e, s0):
-            t_ = keep.tile([P, 2, H], I32, name=f"w1_{e}_{s0}", align_bytes=64)
-            nc.sync.dma_start(t_[:], w1_words[e, s0 : s0 + 2].rearrange("s p i d -> p s (i d)").bitcast(I32))
-            for s in range(2):
+        def load_w1(e, s0, count=2):
+            t_ = keep.tile([P, count, H], I32, name=f"w1_{e}_{s0}", align_bytes=64)
+            nc.sync.dma_start(t_[:], w1_words[e, s0 : s0 + count].rearrange("s p i d -> p s (i d)").bitcast(I32))
+            for s in range(count):
                 w1[e, s0 + s] = t_[:, s, :]
 
         gates = []
@@ -74,14 +73,14 @@ def tile_moe_sdn_lin_relu_kernel(tc, x_words, x_scales, w1_words, w1_scales, w2_
             nc.sync.dma_start(x_plane[32 * q : 32 * q + 16, :].bitcast(I32), x_scales[:, 4 * q : 4 * q + 4, :].bitcast(I32))
         load_tokens(0)
         load_tokens(1)
-        load_w1_scales(0)
         load_w1(0, 0)
         load_tokens(2)
+        load_w1_scales(0)
         load_tokens(3)
         load_w1(0, 2)
         for e in range(1, E):
-            load_w1_scales(e)
             load_w1(e, 0)
+            load_w1_scales(e)
             load_w1(e, 2)
             if e % 2 == 1:
                 load_gate(e // 2)
@@ -97,19 +96,19 @@ def tile_moe_sdn_lin_relu_kernel(tc, x_words, x_scales, w1_words, w1_scales, w2_
             nc.vector.tensor_copy(plane[:], x_plane[:].indirect(offsets[:, half * HALF // 16 : (half + 1) * HALF // 16]))
             slot_plane[half] = plane
 
-        def gather_words(half, s):
-            t_ = keep.tile([P, HALF], U32, name=f"slot_words{half}_{s}", align_bytes=64)
-            nc.vector.tensor_copy(t_[:], x_tok[s][:].bitcast(U32).indirect(offsets[:, half * HALF // 16 : (half + 1) * HALF // 16]))
-            slot_words[half, s] = t_
+        def gather_words(s, e0, e1):
+            t_ = keep.tile([P, (e1 - e0) * C], U32, name=f"slot_words{s}_{e0}", align_bytes=64)
+            nc.vector.tensor_copy(t_[:], x_tok[s][:].bitcast(U32).indirect(offsets[:, e0 * C // 16 : e1 * C // 16]))
+            for e in range(e0, e1):
+                slot_words[e, s] = t_[:, (e - e0) * C : (e - e0 + 1) * C]
 
+        gather_words(0, 0, 2)
         gather_scales(0)
-        gather_words(0, 0)
-        gather_words(0, 1)
+        for s in range(1, PASSES):
+            gather_words(s, 0, 2)
         gather_scales(1)
-        gather_words(0, 2)
-        gather_words(0, 3)
         for s in range(PASSES):
-            gather_words(1, s)
+            gather_words(s, 2, 4)
 
         by_slot = [keep.tile([P, 4, HALF], F32, name=f"by_slot{half}") for half in range(2)]
         by_token = [keep.tile([P, 2 * T if d == 2 else T], F32, name=f"by_token{d}") for d in range(4)]
@@ -117,12 +116,12 @@ def tile_moe_sdn_lin_relu_kernel(tc, x_words, x_scales, w1_words, w1_scales, w2_
         for e in range(E):
             half, c0 = divmod(e * C, HALF)
             acc = [banks.tile([P, H], F32, name="bank") for j in range(2)]
-            for s in range(PASSES):
-                for j in range(2):
+            for s0 in (0, 2):
+                for j, s in ((0, s0), (0, s0 + 1), (1, s0), (1, s0 + 1)):
                     slots = slice(c0 + j * P, c0 + (j + 1) * P)
                     nc.tensor.matmul_mx(
                         out=acc[j][:],
-                        lhsT=slot_words[half, s][:, slots].bitcast(FP8X4),
+                        lhsT=slot_words[e, s][:, j * P : (j + 1) * P].bitcast(FP8X4),
                         lhsT_scale=slot_plane[half][4 * s :, slots],
                         rhs=w1[e, s].bitcast(FP8X4),
                         rhs_scale=w1_plane[e][4 * s :, :],
@@ -145,22 +144,41 @@ def tile_moe_sdn_lin_relu_kernel(tc, x_words, x_scales, w1_words, w1_scales, w2_
             nc.vector.tensor_tensor(by_token[d][:].indirect(cols), by_slot[half][:, d, c0:c1], gates[half][:, c0:c1], MULT)
 
         grouped = [keep.tile([P, width, 4], BF16, name=f"grouped{n}", align_bytes=64) for n, (t0, width, per_bank) in enumerate(CHUNKS)]
-        for c0 in (0, C):
-            for d in range(4):
-                scatter(d, 0, c0, c0 + C)
+        for c0 in (0, P):
+            for d in (0, 1, 3):
+                scatter(d, 0, c0, c0 + P)
+        scatter(2, 0, 0, C)
+        for d in range(4):
+            scatter(d, 0, C, HALF)
         scatter(3, 1, 0, HALF)
         nc.scalar.copy(by_token[2][:, T : 2 * T], by_token[3][:])
         for d in range(2):
             scatter(d, 1, 0, HALF)
             for n, (t0, width, per_bank) in enumerate(CHUNKS):
                 nc.scalar.copy(grouped[n][:, :, d], by_token[d][:, t0 : t0 + width])
+        warm = banks.tile([P, H], F32, name="bank")
+        nc.tensor.transpose(warm[:, 0:P], by_token[1][:, 0:P], ident[:])
+        for s in range(8):
+            nc.tensor.matmul_mx(
+                out=warm[:],
+                lhsT=slot_words[0, 0][:, 0:P].bitcast(FP8X4),
+                lhsT_scale=slot_plane[0][:, 0:P],
+                rhs=w1[0, 0].bitcast(FP8X4),
+                rhs_scale=w1_plane[0][:],
+                start=True,
+                stop=True,
+            )
         scatter(2, 1, 0, HALF)
         upper = by_token[2][:].rearrange("p (u t) -> p t u", u=2)
         codes, scales = [], []
 
         def interleave(n):
             t0, width, per_bank = CHUNKS[n]
-            nc.vector.tensor_copy(grouped[n][:, :, 2:4], upper[:, t0 : t0 + width, :])
+            if n == 3:
+                nc.scalar.copy(grouped[n][:, 0:256, 2:4], upper[:, t0 : t0 + 256, :])
+                nc.vector.tensor_copy(grouped[n][:, 256:512, 2:4], upper[:, t0 + 256 : t0 + 512, :])
+            else:
+                nc.vector.tensor_copy(grouped[n][:, :, 2:4], upper[:, t0 : t0 + width, :])
 
         def quantise(n):
             width = CHUNKS[n][1]
@@ -175,8 +193,8 @@ def tile_moe_sdn_lin_relu_kernel(tc, x_words, x_scales, w1_words, w1_scales, w2_
         quantise(0)
         interleave(2)
         quantise(1)
-        quantise(2)
         interleave(3)
+        quantise(2)
         quantise(3)
 
         rows = out.rearrange("(m p) t -> p m t", p=P)

@@ -69,15 +69,16 @@ def tile_moe_sdn_lin_relu_kernel(tc, x_words, x_scales, w1_words, w1_scales, w2_
             nc.sync.dma_start(t_[:], gate[:, half * HALF : (half + 1) * HALF])
             gates.append(t_)
 
+        load_tokens(0)
         for q in range(4):
             nc.sync.dma_start(x_plane[32 * q : 32 * q + 16, :].bitcast(I32), x_scales[:, 4 * q : 4 * q + 4, :].bitcast(I32))
-        load_tokens(0)
         load_tokens(1)
         load_w1(0, 0)
-        load_tokens(2)
         load_w1_scales(0)
+        load_tokens(2)
+        load_w1(0, 2, 1)
         load_tokens(3)
-        load_w1(0, 2)
+        load_w1(0, 3, 1)
         for e in range(1, E):
             load_w1(e, 0)
             load_w1_scales(e)
@@ -104,10 +105,13 @@ def tile_moe_sdn_lin_relu_kernel(tc, x_words, x_scales, w1_words, w1_scales, w2_
 
         gather_words(0, 0, 2)
         gather_scales(0)
-        for s in range(1, PASSES):
-            gather_words(s, 0, 2)
+        gather_words(1, 0, 2)
+        gather_words(0, 2, 4)
+        gather_words(2, 0, 2)
+        gather_words(3, 0, 1)
+        gather_words(3, 1, 2)
         gather_scales(1)
-        for s in range(PASSES):
+        for s in range(1, PASSES):
             gather_words(s, 2, 4)
 
         by_slot = [keep.tile([P, 4, HALF], F32, name=f"by_slot{half}") for half in range(2)]
@@ -116,8 +120,8 @@ def tile_moe_sdn_lin_relu_kernel(tc, x_words, x_scales, w1_words, w1_scales, w2_
         for e in range(E):
             half, c0 = divmod(e * C, HALF)
             acc = [banks.tile([P, H], F32, name="bank") for j in range(2)]
-            for s0 in (0, 2):
-                for j, s in ((0, s0), (0, s0 + 1), (1, s0), (1, s0 + 1)):
+            for j in range(2):
+                for s in range(PASSES):
                     slots = slice(c0 + j * P, c0 + (j + 1) * P)
                     nc.tensor.matmul_mx(
                         out=acc[j][:],
@@ -150,10 +154,12 @@ def tile_moe_sdn_lin_relu_kernel(tc, x_words, x_scales, w1_words, w1_scales, w2_
         scatter(2, 0, 0, C)
         for d in range(4):
             scatter(d, 0, C, HALF)
-        scatter(3, 1, 0, HALF)
+        scatter(3, 1, 0, C)
+        scatter(0, 1, 0, C)
+        scatter(3, 1, C, HALF)
         nc.scalar.copy(by_token[2][:, T : 2 * T], by_token[3][:])
         for d in range(2):
-            scatter(d, 1, 0, HALF)
+            scatter(d, 1, C if d == 0 else 0, HALF)
             for n, (t0, width, per_bank) in enumerate(CHUNKS):
                 nc.scalar.copy(grouped[n][:, :, d], by_token[d][:, t0 : t0 + width])
         warm = banks.tile([P, H], F32, name="bank")

@@ -14,7 +14,6 @@ U16 = mybir.dt.uint16
 U8 = mybir.dt.uint8
 FP8X4 = mybir.dt.float8_e4m3fn_x4
 FP4X4 = mybir.dt.float4_e2m1fn_x4
-MULT = mybir.AluOpType.mult
 ACT = mybir.ActivationFunctionType
 
 P = 128
@@ -62,12 +61,8 @@ def tile_moe_sdn_lin_relu_kernel(tc, x_words, x_scales, w1_words, w1_scales, w2_
             for s in range(count):
                 w1[e, s0 + s] = t_[:, s, :]
 
-        gates = []
-
-        def load_gate(half):
-            t_ = keep.tile([P, HALF], F32, name=f"gate{half}")
-            nc.sync.dma_start(t_[:], gate[:, half * HALF : (half + 1) * HALF])
-            gates.append(t_)
+        gate_rows = keep.tile([P, P], F32, name="gate_rows")
+        nc.gpsimd.memset(gate_rows[:], 0.0)
 
         load_tokens(0)
         for q in range(4):
@@ -75,6 +70,7 @@ def tile_moe_sdn_lin_relu_kernel(tc, x_words, x_scales, w1_words, w1_scales, w2_
         load_tokens(1)
         load_w1(0, 0)
         load_w1_scales(0)
+        nc.sync.dma_start(gate_rows[0 : E * C // P, :], gate[0].rearrange("(c p) -> c p", p=P))
         load_tokens(2)
         load_w1(0, 2, 1)
         load_tokens(3)
@@ -83,8 +79,6 @@ def tile_moe_sdn_lin_relu_kernel(tc, x_words, x_scales, w1_words, w1_scales, w2_
             load_w1(e, 0)
             load_w1_scales(e)
             load_w1(e, 2)
-            if e % 2 == 1:
-                load_gate(e // 2)
         w2 = keep.tile([P, 2 * N], U8, name="w2", align_bytes=64)
         nc.sync.dma_start(w2[:].bitcast(I32), w2_words[0].bitcast(I32))
         for q in range(4):
@@ -114,8 +108,13 @@ def tile_moe_sdn_lin_relu_kernel(tc, x_words, x_scales, w1_words, w1_scales, w2_
         for s in range(1, PASSES):
             gather_words(s, 2, 4)
 
-        by_slot = [keep.tile([P, 4, HALF], F32, name=f"by_slot{half}") for half in range(2)]
-        by_token = [keep.tile([P, 2 * T if d == 2 else T], F32, name=f"by_token{d}") for d in range(4)]
+        gate_turn = turned.tile([P, P], F32, name="turn")
+        nc.tensor.transpose(gate_turn[:], gate_rows[:], ident[:])
+        gate_cols = keep.tile([P, E * C // P], F32, name="gate_cols")
+        nc.scalar.copy(gate_cols[:], gate_turn[:, 0 : E * C // P])
+
+        by_slot = [keep.tile([P, 2, HALF], F32, name=f"by_slot{half}") for half in range(2)]
+        by_token = [keep.tile([P, T], F32, name=f"by_token{u}") for u in range(2)]
 
         for e in range(E):
             half, c0 = divmod(e * C, HALF)
@@ -132,65 +131,44 @@ def tile_moe_sdn_lin_relu_kernel(tc, x_words, x_scales, w1_words, w1_scales, w2_
                         start=(s == 0),
                         stop=(s == PASSES - 1),
                     )
-            pos, turn = [], []
+            turn = turned.tile([P, 2, C], F32, name="turn")
+            pairs = []
             for j in range(2):
-                pos.append(ring.tile([P, 4, P], F32, name="pos"))
-                nc.scalar.activation(pos[j][:], acc[j][:].rearrange("s (p d) -> s d p", d=4), ACT.Relu)
+                pos = ring.tile([P, 2, P, 2], F32, name="pos")
+                nc.scalar.activation(pos[:], acc[j][:].rearrange("s (p u d) -> s u p d", u=2, d=2), ACT.Relu)
+                gated = ring.tile([P, H], BF16, name="gated")
+                nc.scalar.activation(gated[:], pos[:].rearrange("s u p d -> s (u p d)"), ACT.Copy, scale=gate_cols[:, 2 * e + j : 2 * e + j + 1])
+                pairs.append(gated[:].bitcast(F32))
             for j in range(2):
-                turn.append(turned.tile([P, 4, P], F32, name="turn"))
-                for d in range(4):
-                    nc.tensor.transpose(turn[j][:, d, :], pos[j][:, d, :], ident[:])
-            for j in range(2):
-                nc.scalar.copy(by_slot[half][:, :, c0 + j * P : c0 + (j + 1) * P], turn[j][:])
+                for u in range(2):
+                    nc.tensor.transpose(turn[:, u, j * P : (j + 1) * P], pairs[j][:, u * P : (u + 1) * P], ident[:])
+            nc.scalar.copy(by_slot[half][:, :, c0 : c0 + C], turn[:])
 
-        def scatter(d, half, c0, c1):
+        def scatter(u, half, c0, c1):
             cols = offsets[:, (half * HALF + c0) // 16 : (half * HALF + c1) // 16]
-            nc.vector.tensor_tensor(by_token[d][:].indirect(cols), by_slot[half][:, d, c0:c1], gates[half][:, c0:c1], MULT)
+            nc.vector.tensor_copy(by_token[u][:].indirect(cols), by_slot[half][:, u, c0:c1])
 
-        grouped = [keep.tile([P, width, 4], BF16, name=f"grouped{n}", align_bytes=64) for n, (t0, width, per_bank) in enumerate(CHUNKS)]
-        for c0 in (0, P):
-            for d in (0, 1, 3):
-                scatter(d, 0, c0, c0 + P)
-        scatter(2, 0, 0, C)
-        for d in range(4):
-            scatter(d, 0, C, HALF)
-        scatter(3, 1, 0, C)
+        grouped = [keep.tile([P, width, 2], F32, name=f"grouped{n}", align_bytes=64) for n, (t0, width, per_bank) in enumerate(CHUNKS)]
+        for c0 in (0, C):
+            for u in range(2):
+                scatter(u, 0, c0, c0 + C)
         scatter(0, 1, 0, C)
-        scatter(3, 1, C, HALF)
-        nc.scalar.copy(by_token[2][:, T : 2 * T], by_token[3][:])
-        for d in range(2):
-            scatter(d, 1, C if d == 0 else 0, HALF)
-            for n, (t0, width, per_bank) in enumerate(CHUNKS):
-                nc.scalar.copy(grouped[n][:, :, d], by_token[d][:, t0 : t0 + width])
-        warm = banks.tile([P, H], F32, name="bank")
-        nc.tensor.transpose(warm[:, 0:P], by_token[1][:, 0:P], ident[:])
-        for s in range(8):
-            nc.tensor.matmul_mx(
-                out=warm[:],
-                lhsT=slot_words[0, 0][:, 0:P].bitcast(FP8X4),
-                lhsT_scale=slot_plane[0][:, 0:P],
-                rhs=w1[0, 0].bitcast(FP8X4),
-                rhs_scale=w1_plane[0][:],
-                start=True,
-                stop=True,
-            )
-        scatter(2, 1, 0, HALF)
-        upper = by_token[2][:].rearrange("p (u t) -> p t u", u=2)
+        scatter(1, 1, 0, P)
+        scatter(0, 1, C, HALF)
+        for n, (t0, width, per_bank) in enumerate(CHUNKS):
+            nc.scalar.copy(grouped[n][:, :, 0], by_token[0][:, t0 : t0 + width])
+        scatter(1, 1, P, HALF)
         codes, scales = [], []
 
         def interleave(n):
             t0, width, per_bank = CHUNKS[n]
-            if n == 3:
-                nc.scalar.copy(grouped[n][:, 0:256, 2:4], upper[:, t0 : t0 + 256, :])
-                nc.vector.tensor_copy(grouped[n][:, 256:512, 2:4], upper[:, t0 + 256 : t0 + 512, :])
-            else:
-                nc.vector.tensor_copy(grouped[n][:, :, 2:4], upper[:, t0 : t0 + width, :])
+            nc.vector.tensor_copy(grouped[n][:, :, 1], by_token[1][:, t0 : t0 + width])
 
         def quantise(n):
             width = CHUNKS[n][1]
             c_ = keep.tile([P, width], U32, name=f"codes{n}", align_bytes=64)
             s_ = keep.tile([P, width], U8, name=f"scales{n}", align_bytes=64)
-            nc.vector.quantize_mx(out=c_[:].bitcast(FP8X4), scales=s_[:], in_=grouped[n][:].rearrange("p t d -> p (t d)"))
+            nc.vector.quantize_mx(out=c_[:].bitcast(FP8X4), scales=s_[:], in_=grouped[n][:].rearrange("p t u -> p (t u)").bitcast(BF16))
             codes.append(c_)
             scales.append(s_)
 

@@ -27,8 +27,7 @@ def tile_moe_sdn_lin_relu_kernel(tc, x_words, x_scales, w1_words, w1_scales, w2_
     with ExitStack() as ctx:
         keep = ctx.enter_context(tc.tile_pool(name="keep", bufs=1))
         ring = ctx.enter_context(tc.tile_pool(name="ring", bufs=4))
-        banks = ctx.enter_context(tc.psum_pool(name="banks", bufs=5))
-        turned = ctx.enter_context(tc.psum_pool(name="turned", bufs=3))
+        banks = ctx.enter_context(tc.psum_pool(name="banks", bufs=1))
 
         offsets = keep.tile([P, E * C // 16], U16, name="offsets")
         nc.sync.dma_start(offsets[:], offs)
@@ -55,7 +54,7 @@ def tile_moe_sdn_lin_relu_kernel(tc, x_words, x_scales, w1_words, w1_scales, w2_
             for q in range(4):
                 nc.sync.dma_start(w1_plane[e][32 * q : 32 * q + 16, :].bitcast(I32), w1_scales[e, :, 4 * q : 4 * q + 4, :].bitcast(I32))
 
-        def load_w1(e, s0, count=2):
+        def load_w1(e, s0, count):
             t_ = keep.tile([P, count, H], I32, name=f"w1_{e}_{s0}", align_bytes=64)
             nc.sync.dma_start(t_[:], w1_words[e, s0 : s0 + count].rearrange("s p i d -> p s (i d)").bitcast(I32))
             for s in range(count):
@@ -67,18 +66,16 @@ def tile_moe_sdn_lin_relu_kernel(tc, x_words, x_scales, w1_words, w1_scales, w2_
         load_tokens(0)
         for q in range(4):
             nc.sync.dma_start(x_plane[32 * q : 32 * q + 16, :].bitcast(I32), x_scales[:, 4 * q : 4 * q + 4, :].bitcast(I32))
-        load_tokens(1)
-        load_w1(0, 0)
+        for s in range(1, PASSES):
+            load_tokens(s)
         load_w1_scales(0)
+        for s in range(PASSES):
+            load_w1(0, s, 1)
         nc.sync.dma_start(gate_rows[0 : E * C // P, :], gate[0].rearrange("(c p) -> c p", p=P))
-        load_tokens(2)
-        load_w1(0, 2, 1)
-        load_tokens(3)
-        load_w1(0, 3, 1)
         for e in range(1, E):
-            load_w1(e, 0)
+            load_w1(e, 0, 2)
             load_w1_scales(e)
-            load_w1(e, 2)
+            load_w1(e, 2, 2)
         w2 = keep.tile([P, 2 * N], U8, name="w2", align_bytes=64)
         nc.sync.dma_start(w2[:].bitcast(I32), w2_words[0].bitcast(I32))
         for q in range(4):
@@ -86,29 +83,24 @@ def tile_moe_sdn_lin_relu_kernel(tc, x_words, x_scales, w1_words, w1_scales, w2_
 
         slot_words, slot_plane = {}, {}
 
-        def gather_scales(half):
-            plane = keep.tile([P, HALF], U8, name=f"slot_plane{half}", align_bytes=64)
+        def gather_scales(half, tag):
+            plane = keep.tile([P, HALF], U8, name=tag, align_bytes=64)
             nc.vector.tensor_copy(plane[:], x_plane[:].indirect(offsets[:, half * HALF // 16 : (half + 1) * HALF // 16]))
             slot_plane[half] = plane
 
-        def gather_words(s, e0, e1):
-            t_ = keep.tile([P, (e1 - e0) * C], U32, name=f"slot_words{s}_{e0}", align_bytes=64)
+        def gather_words(s, e0, e1, tag):
+            t_ = keep.tile([P, (e1 - e0) * C], U32, name=tag, align_bytes=64)
             nc.vector.tensor_copy(t_[:], x_tok[s][:].bitcast(U32).indirect(offsets[:, e0 * C // 16 : e1 * C // 16]))
             for e in range(e0, e1):
                 slot_words[e, s] = t_[:, (e - e0) * C : (e - e0 + 1) * C]
 
-        gather_words(0, 0, 2)
-        gather_scales(0)
-        gather_words(1, 0, 2)
-        gather_words(0, 2, 4)
-        gather_words(2, 0, 2)
-        gather_words(3, 0, 1)
-        gather_words(3, 1, 2)
-        gather_scales(1)
+        gather_words(0, 0, 2, "slot_words0")
+        gather_scales(0, "slot_plane0")
+        gather_scales(1, "slot_plane1")
         for s in range(1, PASSES):
-            gather_words(s, 2, 4)
+            gather_words(s, 0, 2, f"slot_words{s}")
 
-        gate_turn = turned.tile([P, P], F32, name="turn")
+        gate_turn = banks.tile([P, P], F32, name="bank7")
         nc.tensor.transpose(gate_turn[:], gate_rows[:], ident[:])
         gate_cols = keep.tile([P, E * C // P], F32, name="gate_cols")
         nc.scalar.copy(gate_cols[:], gate_turn[:, 0 : E * C // P])
@@ -116,33 +108,53 @@ def tile_moe_sdn_lin_relu_kernel(tc, x_words, x_scales, w1_words, w1_scales, w2_
         by_slot = [keep.tile([P, 2, HALF], F32, name=f"by_slot{half}") for half in range(2)]
         by_token = [keep.tile([P, T], F32, name=f"by_token{u}") for u in range(2)]
 
-        for e in range(E):
+        acc, pos, pairs = {}, {}, {}
+
+        def multiply(e):
             half, c0 = divmod(e * C, HALF)
-            acc = [banks.tile([P, H], F32, name="bank") for j in range(2)]
             for j in range(2):
-                for s in range(PASSES):
-                    slots = slice(c0 + j * P, c0 + (j + 1) * P)
+                acc[e, j] = banks.tile([P, H], F32, name=f"bank{2 * e + j}")
+            for s in range(PASSES):
+                for j in range(2):
                     nc.tensor.matmul_mx(
-                        out=acc[j][:],
+                        out=acc[e, j][:],
                         lhsT=slot_words[e, s][:, j * P : (j + 1) * P].bitcast(FP8X4),
-                        lhsT_scale=slot_plane[half][4 * s :, slots],
+                        lhsT_scale=slot_plane[half][4 * s :, c0 + j * P : c0 + (j + 1) * P],
                         rhs=w1[e, s].bitcast(FP8X4),
                         rhs_scale=w1_plane[e][4 * s :, :],
                         start=(s == 0),
                         stop=(s == PASSES - 1),
                     )
-            turn = turned.tile([P, 2, C], F32, name="turn")
-            pairs = []
-            for j in range(2):
-                pos = ring.tile([P, 2, P, 2], F32, name="pos")
-                nc.scalar.activation(pos[:], acc[j][:].rearrange("s (p u d) -> s u p d", u=2, d=2), ACT.Relu)
-                gated = ring.tile([P, H], BF16, name="gated")
-                nc.scalar.activation(gated[:], pos[:].rearrange("s u p d -> s (u p d)"), ACT.Copy, scale=gate_cols[:, 2 * e + j : 2 * e + j + 1])
-                pairs.append(gated[:].bitcast(F32))
+
+        def rectify(e, j):
+            pos[e, j] = ring.tile([P, 2, P, 2], F32, name="pos")
+            nc.scalar.activation(pos[e, j][:], acc[e, j][:].rearrange("s (p u d) -> s u p d", u=2, d=2), ACT.Relu)
+
+        def weigh(e, j):
+            gated = ring.tile([P, H], BF16, name="gated")
+            nc.scalar.activation(gated[:], pos[e, j][:].rearrange("s u p d -> s (u p d)"), ACT.Copy, scale=gate_cols[:, 2 * e + j : 2 * e + j + 1])
+            pairs[e, j] = gated[:].bitcast(F32)
+
+        def turn(e):
+            half, c0 = divmod(e * C, HALF)
+            turned = banks.tile([P, 2, C], F32, name=f"bank{2 * (e + 1) % 8}")
             for j in range(2):
                 for u in range(2):
-                    nc.tensor.transpose(turn[:, u, j * P : (j + 1) * P], pairs[j][:, u * P : (u + 1) * P], ident[:])
-            nc.scalar.copy(by_slot[half][:, :, c0 : c0 + C], turn[:])
+                    nc.tensor.transpose(turned[:, u, j * P : (j + 1) * P], pairs[e, j][:, u * P : (u + 1) * P], ident[:])
+            nc.scalar.copy(by_slot[half][:, :, c0 : c0 + C], turned[:])
+
+        for e in range(E):
+            multiply(e)
+            if e == 0:
+                for s in range(PASSES):
+                    gather_words(s, 2, 4, f"w1_0_{s}")
+            rectify(e, 0)
+            if e > 0:
+                turn(e - 1)
+            weigh(e, 0)
+            rectify(e, 1)
+            weigh(e, 1)
+        turn(E - 1)
 
         def scatter(u, half, c0, c1):
             cols = offsets[:, (half * HALF + c0) // 16 : (half * HALF + c1) // 16]
@@ -185,7 +197,7 @@ def tile_moe_sdn_lin_relu_kernel(tc, x_words, x_scales, w1_words, w1_scales, w2_
         count = 0
         for n, (t0, width, per_bank) in enumerate(CHUNKS):
             for m0 in range(0, N // P, per_bank):
-                bank = banks.tile([P, H], F32, name="bank")
+                bank = banks.tile([P, H], F32, name=f"bank{(count + 1) % 8}")
                 for m in range(m0, m0 + per_bank):
                     nc.tensor.matmul_mx(
                         out=bank[:, (m - m0) * width : (m - m0 + 1) * width],

@@ -35,9 +35,8 @@ def tile_moe_sdn_lin_relu_kernel(tc, x_words, x_scales, w1_words, w1_scales, w2_
         x_plane = keep.tile([P, T], U8, name="x_plane", align_bytes=64)
         w1_plane = [keep.tile([P, H], U8, name=f"w1_plane{e}", align_bytes=64) for e in range(E)]
         w2_plane = keep.tile([P, N], U8, name="w2_plane", align_bytes=64)
-        nc.vector.memset(x_plane[:].bitcast(I32), 0)
-        nc.gpsimd.memset(w1_plane[0][:].bitcast(I32), 0)
-        for e in range(1, E):
+        nc.gpsimd.memset(x_plane[:].bitcast(I32), 0)
+        for e in range(E):
             nc.vector.memset(w1_plane[e][:].bitcast(I32), 0)
         nc.vector.memset(w2_plane[:].bitcast(I32), 0)
         ident = keep.tile([P, P], F32, name="ident")
@@ -54,7 +53,7 @@ def tile_moe_sdn_lin_relu_kernel(tc, x_words, x_scales, w1_words, w1_scales, w2_
             for q in range(4):
                 nc.sync.dma_start(w1_plane[e][32 * q : 32 * q + 16, :].bitcast(I32), w1_scales[e, :, 4 * q : 4 * q + 4, :].bitcast(I32))
 
-        def load_w1(e, s0, count):
+        def load_w1(e, s0, count=2):
             t_ = keep.tile([P, count, H], I32, name=f"w1_{e}_{s0}", align_bytes=64)
             nc.sync.dma_start(t_[:], w1_words[e, s0 : s0 + count].rearrange("s p i d -> p s (i d)").bitcast(I32))
             for s in range(count):
@@ -66,16 +65,23 @@ def tile_moe_sdn_lin_relu_kernel(tc, x_words, x_scales, w1_words, w1_scales, w2_
         load_tokens(0)
         for q in range(4):
             nc.sync.dma_start(x_plane[32 * q : 32 * q + 16, :].bitcast(I32), x_scales[:, 4 * q : 4 * q + 4, :].bitcast(I32))
-        for s in range(1, PASSES):
-            load_tokens(s)
+        load_w1(0, 0, 2)
+        load_tokens(1)
         load_w1_scales(0)
-        for s in range(PASSES):
-            load_w1(0, s, 1)
+        load_tokens(2)
+        load_tokens(3)
+        load_w1(0, 2, 1)
+        load_w1(0, 3, 1)
         nc.sync.dma_start(gate_rows[0 : E * C // P, :], gate[0].rearrange("(c p) -> c p", p=P))
-        for e in range(1, E):
-            load_w1(e, 0, 2)
-            load_w1_scales(e)
-            load_w1(e, 2, 2)
+        load_w1(1, 0, 2)
+        load_w1_scales(1)
+        load_w1(1, 2, 2)
+        load_w1(2, 0, 2)
+        load_w1_scales(2)
+        load_w1(2, 2, 2)
+        load_w1(3, 0, 2)
+        load_w1_scales(3)
+        load_w1(3, 2, 2)
         w2 = keep.tile([P, 2 * N], U8, name="w2", align_bytes=64)
         nc.sync.dma_start(w2[:].bitcast(I32), w2_words[0].bitcast(I32))
         for q in range(4):
@@ -88,17 +94,20 @@ def tile_moe_sdn_lin_relu_kernel(tc, x_words, x_scales, w1_words, w1_scales, w2_
             nc.vector.tensor_copy(plane[:], x_plane[:].indirect(offsets[:, half * HALF // 16 : (half + 1) * HALF // 16]))
             slot_plane[half] = plane
 
-        def gather_words(s, e0, e1, tag):
-            t_ = keep.tile([P, (e1 - e0) * C], U32, name=tag, align_bytes=64)
-            nc.vector.tensor_copy(t_[:], x_tok[s][:].bitcast(U32).indirect(offsets[:, e0 * C // 16 : e1 * C // 16]))
-            for e in range(e0, e1):
-                slot_words[e, s] = t_[:, (e - e0) * C : (e - e0 + 1) * C]
+        def gather_words(e0, e1, s0, count, tag):
+            t_ = keep.tile([P, count, (e1 - e0) * C], U32, name=tag, align_bytes=64)
+            for s in range(s0, s0 + count):
+                nc.vector.tensor_copy(t_[:, s - s0, :], x_tok[s][:].bitcast(U32).indirect(offsets[:, e0 * C // 16 : e1 * C // 16]))
+                for e in range(e0, e1):
+                    slot_words[e, s] = t_[:, s - s0, (e - e0) * C : (e - e0 + 1) * C]
 
-        gather_words(0, 0, 2, "slot_words0")
-        gather_scales(0, "slot_plane0")
-        gather_scales(1, "slot_plane1")
-        for s in range(1, PASSES):
-            gather_words(s, 0, 2, f"slot_words{s}")
+        for s in range(PASSES - 1):
+            gather_words(0, 2, s, 1, f"slot_words{s}")
+            if s == 0:
+                gather_scales(0, "slot_plane0")
+                gather_scales(1, "slot_plane1")
+        for e in range(2):
+            gather_words(e, e + 1, PASSES - 1, 1, f"last_words{e}")
 
         gate_turn = banks.tile([P, P], F32, name="bank7")
         nc.tensor.transpose(gate_turn[:], gate_rows[:], ident[:])
@@ -110,12 +119,16 @@ def tile_moe_sdn_lin_relu_kernel(tc, x_words, x_scales, w1_words, w1_scales, w2_
 
         acc, pos, pairs = {}, {}, {}
 
-        def multiply(e):
+        def multiply(e, s0):
             half, c0 = divmod(e * C, HALF)
-            for j in range(2):
-                acc[e, j] = banks.tile([P, H], F32, name=f"bank{2 * e + j}")
-            for s in range(PASSES):
+            steps = [(s, j) for s in range(s0, s0 + 2) for j in range(2)]
+            if s0 == 0:
                 for j in range(2):
+                    acc[e, j] = banks.tile([P, H], F32, name=f"bank{2 * e + j}")
+            else:
+                steps = sorted(steps, key=lambda step: step[1])
+            if True:
+                for s, j in steps:
                     nc.tensor.matmul_mx(
                         out=acc[e, j][:],
                         lhsT=slot_words[e, s][:, j * P : (j + 1) * P].bitcast(FP8X4),
@@ -137,24 +150,41 @@ def tile_moe_sdn_lin_relu_kernel(tc, x_words, x_scales, w1_words, w1_scales, w2_
 
         def turn(e):
             half, c0 = divmod(e * C, HALF)
-            turned = banks.tile([P, 2, C], F32, name=f"bank{2 * (e + 1) % 8}")
+            turned = banks.tile([P, 2, C], F32, name=f"bank{(2,0,6,1)[e]}")
             for j in range(2):
                 for u in range(2):
                     nc.tensor.transpose(turned[:, u, j * P : (j + 1) * P], pairs[e, j][:, u * P : (u + 1) * P], ident[:])
             nc.scalar.copy(by_slot[half][:, :, c0 : c0 + C], turned[:])
 
-        for e in range(E):
-            multiply(e)
-            if e == 0:
-                for s in range(PASSES):
-                    gather_words(s, 2, 4, f"w1_0_{s}")
-            rectify(e, 0)
-            if e > 0:
-                turn(e - 1)
-            weigh(e, 0)
-            rectify(e, 1)
-            weigh(e, 1)
-        turn(E - 1)
+        multiply(0,0)
+        multiply(0,2)
+        gather_words(2,4,0,4,"w1_0_2")
+        rectify(0,0)
+        rectify(0,1)
+        weigh(0,0)
+        weigh(0,1)
+        multiply(1,0)
+        multiply(1,2)
+        rectify(1,0)
+        rectify(1,1)
+        weigh(1,0)
+        turn(0)
+        weigh(1,1)
+        turn(1)
+        multiply(2,0)
+        multiply(2,2)
+        multiply(3,0)
+        multiply(3,2)
+        rectify(2,0)
+        rectify(2,1)
+        weigh(2,0)
+        weigh(2,1)
+        rectify(3,0)
+        rectify(3,1)
+        turn(2)
+        weigh(3,0)
+        weigh(3,1)
+        turn(3)
 
         def scatter(u, half, c0, c1):
             cols = offsets[:, (half * HALF + c0) // 16 : (half * HALF + c1) // 16]

@@ -76,12 +76,10 @@ def tile_moe_sdn_lin_relu_kernel(tc, x_words, x_scales, w1_words, w1_scales, w2_
         load_w1(1, 0, 2)
         load_w1_scales(1)
         load_w1(1, 2, 2)
-        load_w1(2, 0, 2)
+        load_w1(2, 0, 4)
         load_w1_scales(2)
-        load_w1(2, 2, 2)
-        load_w1(3, 0, 2)
+        load_w1(3, 0, 4)
         load_w1_scales(3)
-        load_w1(3, 2, 2)
         w2 = keep.tile([P, 2 * N], U8, name="w2", align_bytes=64)
         nc.sync.dma_start(w2[:].bitcast(I32), w2_words[0].bitcast(I32))
         for q in range(4):
@@ -119,16 +117,12 @@ def tile_moe_sdn_lin_relu_kernel(tc, x_words, x_scales, w1_words, w1_scales, w2_
 
         acc, pos, pairs = {}, {}, {}
 
-        def multiply(e, s0):
+        def multiply(e, tiles, passes):
             half, c0 = divmod(e * C, HALF)
-            steps = [(s, j) for s in range(s0, s0 + 2) for j in range(2)]
-            if s0 == 0:
-                for j in range(2):
-                    acc[e, j] = banks.tile([P, H], F32, name=f"bank{2 * e + j}")
-            else:
-                steps = sorted(steps, key=lambda step: step[1])
-            if True:
-                for s, j in steps:
+            for s in passes:
+                for j in tiles:
+                    if s == 0:
+                        acc[e, j] = banks.tile([P, H], F32, name=f"bank{2 * e + j}")
                     nc.tensor.matmul_mx(
                         out=acc[e, j][:],
                         lhsT=slot_words[e, s][:, j * P : (j + 1) * P].bitcast(FP8X4),
@@ -150,39 +144,40 @@ def tile_moe_sdn_lin_relu_kernel(tc, x_words, x_scales, w1_words, w1_scales, w2_
 
         def turn(e):
             half, c0 = divmod(e * C, HALF)
-            turned = banks.tile([P, 2, C], F32, name=f"bank{(2,0,6,1)[e]}")
+            turned = banks.tile([P, 2, C], F32, name=f"bank{(2,4,6,0)[e]}")
             for j in range(2):
                 for u in range(2):
                     nc.tensor.transpose(turned[:, u, j * P : (j + 1) * P], pairs[e, j][:, u * P : (u + 1) * P], ident[:])
             nc.scalar.copy(by_slot[half][:, :, c0 : c0 + C], turned[:])
 
-        multiply(0,0)
-        multiply(0,2)
+        multiply(0,(0,1),(0,1,2))
         gather_words(2,4,0,4,"w1_0_2")
+        multiply(0,(0,1),(3,))
         rectify(0,0)
         rectify(0,1)
         weigh(0,0)
         weigh(0,1)
-        multiply(1,0)
-        multiply(1,2)
+        multiply(1,(0,1),(0,1))
+        multiply(1,(0,),(2,3))
         rectify(1,0)
-        rectify(1,1)
-        weigh(1,0)
         turn(0)
+        multiply(1,(1,),(2,3))
+        weigh(1,0)
+        rectify(1,1)
         weigh(1,1)
-        turn(1)
-        multiply(2,0)
-        multiply(2,2)
-        multiply(3,0)
-        multiply(3,2)
+        multiply(2,(0,),range(4))
         rectify(2,0)
-        rectify(2,1)
+        turn(1)
+        multiply(2,(1,),range(4))
         weigh(2,0)
+        rectify(2,1)
         weigh(2,1)
+        multiply(3,(0,),range(4))
         rectify(3,0)
-        rectify(3,1)
         turn(2)
+        multiply(3,(1,),range(4))
         weigh(3,0)
+        rectify(3,1)
         weigh(3,1)
         turn(3)
 

@@ -42,12 +42,11 @@ def tile_moe_sdn_lin_relu_kernel(tc, x_words, x_scales, w1_words, w1_scales, w2_
         ident = keep.tile([P, P], F32, name="ident")
         make_identity(nc, ident[:])
 
-        x_tok, w1 = {}, {}
+        x_tok = keep.tile([P, PASSES * T], I32, name="x_tok", align_bytes=64)
+        w1 = {}
 
         def load_tokens(s):
-            t_ = keep.tile([P, T], I32, name=f"x_tok{s}", align_bytes=64)
-            nc.sync.dma_start(t_[:], x_words[s].rearrange("p t d -> p (t d)").bitcast(I32))
-            x_tok[s] = t_
+            nc.sync.dma_start(x_tok[:, s * T : (s + 1) * T], x_words[s].rearrange("p t d -> p (t d)").bitcast(I32))
 
         def load_w1_scales(e):
             for q in range(4):
@@ -65,21 +64,22 @@ def tile_moe_sdn_lin_relu_kernel(tc, x_words, x_scales, w1_words, w1_scales, w2_
         load_tokens(0)
         for q in range(4):
             nc.sync.dma_start(x_plane[32 * q : 32 * q + 16, :].bitcast(I32), x_scales[:, 4 * q : 4 * q + 4, :].bitcast(I32))
-        load_w1(0, 0, 2)
+        nc.sync.dma_start(gate_rows[0 : E * C // P, :], gate[0].rearrange("(c p) -> c p", p=P))
         load_tokens(1)
+        load_w1(0, 0, 2)
         load_w1_scales(0)
         load_tokens(2)
         load_tokens(3)
-        load_w1(0, 2, 1)
-        load_w1(0, 3, 1)
-        nc.sync.dma_start(gate_rows[0 : E * C // P, :], gate[0].rearrange("(c p) -> c p", p=P))
+        load_w1(0, 2, 2)
         load_w1(1, 0, 2)
         load_w1_scales(1)
         load_w1(1, 2, 2)
-        load_w1(2, 0, 4)
+        load_w1(2, 0, 2)
         load_w1_scales(2)
-        load_w1(3, 0, 4)
+        load_w1(2, 2, 2)
+        load_w1(3, 0, 2)
         load_w1_scales(3)
+        load_w1(3, 2, 2)
         w2 = keep.tile([P, 2 * N], U8, name="w2", align_bytes=64)
         nc.sync.dma_start(w2[:].bitcast(I32), w2_words[0].bitcast(I32))
         for q in range(4):
@@ -95,7 +95,7 @@ def tile_moe_sdn_lin_relu_kernel(tc, x_words, x_scales, w1_words, w1_scales, w2_
         def gather_words(e0, e1, s0, count, tag):
             t_ = keep.tile([P, count, (e1 - e0) * C], U32, name=tag, align_bytes=64)
             for s in range(s0, s0 + count):
-                nc.vector.tensor_copy(t_[:, s - s0, :], x_tok[s][:].bitcast(U32).indirect(offsets[:, e0 * C // 16 : e1 * C // 16]))
+                nc.vector.tensor_copy(t_[:, s - s0, :], x_tok[:, s * T : (s + 1 if e0 < 2 else PASSES) * T].bitcast(U32).indirect(offsets[:, e0 * C // 16 : e1 * C // 16]))
                 for e in range(e0, e1):
                     slot_words[e, s] = t_[:, s - s0, (e - e0) * C : (e - e0 + 1) * C]
 
@@ -150,9 +150,8 @@ def tile_moe_sdn_lin_relu_kernel(tc, x_words, x_scales, w1_words, w1_scales, w2_
                     nc.tensor.transpose(turned[:, u, j * P : (j + 1) * P], pairs[e, j][:, u * P : (u + 1) * P], ident[:])
             nc.scalar.copy(by_slot[half][:, :, c0 : c0 + C], turned[:])
 
-        multiply(0,(0,1),(0,1,2))
-        gather_words(2,4,0,4,"w1_0_2")
-        multiply(0,(0,1),(3,))
+        gather_words(2,4,0,4,"late_words")
+        multiply(0,(0,1),range(4))
         rectify(0,0)
         rectify(0,1)
         weigh(0,0)

@@ -191,28 +191,37 @@ def tile_moe_sdn_lin_relu_kernel(tc, x_words, x_scales, w1_words, w1_scales, w2_
         scatter(0, 1, 0, C)
         scatter(1, 1, 0, P)
         scatter(0, 1, C, HALF)
+        staged = {n: keep.tile([P, 2, CHUNKS[n][1]], F32, name=f"staged{n}") for n in (2, 3)}
         for n, (t0, width, per_bank) in enumerate(CHUNKS):
-            nc.scalar.copy(grouped[n][:, :, 0], by_token[0][:, t0 : t0 + width])
+            nc.scalar.copy(staged[n][:, 0, :] if n in staged else grouped[n][:, :, 0], by_token[0][:, t0 : t0 + width])
+        warm = banks.tile([P, H], F32, name="bank0")
+        nc.tensor.transpose(warm[:, 0:P], by_token[0][:, 0:P], ident[:])
+        for s in range(5):
+            nc.tensor.matmul_mx(out=warm[:], lhsT=slot_words[0, 0][:, 0:P].bitcast(FP8X4), lhsT_scale=slot_plane[0][:, 0:P], rhs=w1[0, 0].bitcast(FP8X4), rhs_scale=w1_plane[0][:], start=True, stop=True)
         scatter(1, 1, P, HALF)
-        codes, scales = [], []
+        codes, scales = {}, {}
 
         def interleave(n):
             t0, width, per_bank = CHUNKS[n]
-            nc.vector.tensor_copy(grouped[n][:, :, 1], by_token[1][:, t0 : t0 + width])
+            if n in staged:
+                nc.scalar.copy(staged[n][:, 1, :], by_token[1][:, t0 : t0 + width])
+                nc.vector.tensor_copy(grouped[n][:], staged[n][:].rearrange("p u t -> p t u"))
+            else:
+                nc.vector.tensor_copy(grouped[n][:, :, 1], by_token[1][:, t0 : t0 + width])
 
         def quantise(n):
             width = CHUNKS[n][1]
             c_ = keep.tile([P, width], U32, name=f"codes{n}", align_bytes=64)
             s_ = keep.tile([P, width], U8, name=f"scales{n}", align_bytes=64)
             nc.vector.quantize_mx(out=c_[:].bitcast(FP8X4), scales=s_[:], in_=grouped[n][:].rearrange("p t u -> p (t u)").bitcast(BF16))
-            codes.append(c_)
-            scales.append(s_)
+            codes[n] = c_
+            scales[n] = s_
 
         interleave(0)
         interleave(1)
         quantise(0)
-        interleave(2)
         quantise(1)
+        interleave(2)
         interleave(3)
         quantise(2)
         quantise(3)

@@ -19,7 +19,12 @@ ACT = mybir.ActivationFunctionType
 P = 128
 PASSES = K // 512
 HALF = E * C // 2
-CHUNKS = [(0, 128, 2), (128, 128, 4), (256, 256, 2), (512, 512, 1)]
+BANKS = 8
+PER_COLUMN = 16
+QUADRANT = 32
+RANGES = [(0, 128, 2), (128, 128, 4), (256, 256, 2), (512, 512, 1)]
+DIRECT = 2
+VECTOR_FROM = 4
 
 
 def tile_moe_sdn_lin_relu_kernel(tc, x_words, x_scales, w1_words, w1_scales, w2_words, w2_scales, gate, offs, out):
@@ -29,7 +34,7 @@ def tile_moe_sdn_lin_relu_kernel(tc, x_words, x_scales, w1_words, w1_scales, w2_
         ring = ctx.enter_context(tc.tile_pool(name="ring", bufs=4))
         banks = ctx.enter_context(tc.psum_pool(name="banks", bufs=1))
 
-        offsets = keep.tile([P, E * C // 16], U16, name="offsets")
+        offsets = keep.tile([P, E * C // PER_COLUMN], U16, name="offsets")
         nc.sync.dma_start(offsets[:], offs)
 
         x_plane = keep.tile([P, T], U8, name="x_plane", align_bytes=64)
@@ -48,74 +53,70 @@ def tile_moe_sdn_lin_relu_kernel(tc, x_words, x_scales, w1_words, w1_scales, w2_
         def load_tokens(s):
             nc.sync.dma_start(x_tok[:, s * T : (s + 1) * T], x_words[s].rearrange("p t d -> p (t d)").bitcast(I32))
 
-        def load_w1_scales(e):
+        def load_plane(plane, scale_rows):
+            live = 4 * scale_rows.shape[0]
             for q in range(4):
-                nc.sync.dma_start(w1_plane[e][32 * q : 32 * q + 16, :].bitcast(I32), w1_scales[e, :, 4 * q : 4 * q + 4, :].bitcast(I32))
+                nc.sync.dma_start(plane[QUADRANT * q : QUADRANT * q + live, :].bitcast(I32), scale_rows[:, 4 * q : 4 * q + 4, :].bitcast(I32))
 
-        def load_w1(e, s0, count=2):
-            t_ = keep.tile([P, count, H], I32, name=f"w1_{e}_{s0}", align_bytes=64)
-            nc.sync.dma_start(t_[:], w1_words[e, s0 : s0 + count].rearrange("s p i d -> p s (i d)").bitcast(I32))
-            for s in range(count):
-                w1[e, s0 + s] = t_[:, s, :]
+        def load_w1(e, s0):
+            two = keep.tile([P, 2, H], I32, name=f"w1_{e}_{s0}", align_bytes=64)
+            nc.sync.dma_start(two[:], w1_words[e, s0 : s0 + 2].rearrange("s p i d -> p s (i d)").bitcast(I32))
+            for s in range(2):
+                w1[e, s0 + s] = two[:, s, :]
 
         gate_rows = keep.tile([P, P], F32, name="gate_rows")
         nc.gpsimd.memset(gate_rows[:], 0.0)
 
         load_tokens(0)
-        for q in range(4):
-            nc.sync.dma_start(x_plane[32 * q : 32 * q + 16, :].bitcast(I32), x_scales[:, 4 * q : 4 * q + 4, :].bitcast(I32))
+        load_plane(x_plane, x_scales)
         nc.sync.dma_start(gate_rows[0 : E * C // P, :], gate[0].rearrange("(c p) -> c p", p=P))
         load_tokens(1)
-        load_w1(0, 0, 2)
-        load_w1_scales(0)
-        load_tokens(2)
-        load_tokens(3)
-        load_w1(0, 2, 2)
-        load_w1(1, 0, 2)
-        load_w1_scales(1)
-        load_w1(1, 2, 2)
-        load_w1(2, 0, 2)
-        load_w1_scales(2)
-        load_w1(2, 2, 2)
-        load_w1(3, 0, 2)
-        load_w1_scales(3)
-        load_w1(3, 2, 2)
+        for e in range(E):
+            load_w1(e, 0)
+            load_plane(w1_plane[e], w1_scales[e])
+            if e == 0:
+                load_tokens(2)
+                load_tokens(3)
+            load_w1(e, 2)
         w2 = keep.tile([P, 2 * N], U8, name="w2", align_bytes=64)
         nc.sync.dma_start(w2[:].bitcast(I32), w2_words[0].bitcast(I32))
         for q in range(4):
-            nc.sync.dma_start(w2_plane[32 * q : 32 * q + 4, :].bitcast(I32), w2_scales[0, 4 * q : 4 * q + 4, :].bitcast(I32))
+            nc.sync.dma_start(w2_plane[QUADRANT * q : QUADRANT * q + 4, :].bitcast(I32), w2_scales[0, 4 * q : 4 * q + 4, :].bitcast(I32))
+
+        def slots(first, last):
+            return offsets[:, first // PER_COLUMN : last // PER_COLUMN]
 
         slot_words, slot_plane = {}, {}
 
-        def gather_scales(half, tag):
-            plane = keep.tile([P, HALF], U8, name=tag, align_bytes=64)
-            nc.vector.tensor_copy(plane[:], x_plane[:].indirect(offsets[:, half * HALF // 16 : (half + 1) * HALF // 16]))
-            slot_plane[half] = plane
+        def gather_scales(half):
+            slot_plane[half] = keep.tile([P, HALF], U8, name=f"slot_plane{half}", align_bytes=64)
+            nc.vector.tensor_copy(slot_plane[half][:], x_plane[:].indirect(slots(half * HALF, (half + 1) * HALF)))
 
-        def gather_words(e0, e1, s0, count, tag):
-            t_ = keep.tile([P, count, (e1 - e0) * C], U32, name=tag, align_bytes=64)
-            for s in range(s0, s0 + count):
-                nc.vector.tensor_copy(t_[:, s - s0, :], x_tok[:, s * T : (s + 1 if e0 < 2 else PASSES) * T].bitcast(U32).indirect(offsets[:, e0 * C // 16 : e1 * C // 16]))
+        def gather_words(e0, e1, passes, window_end, tag):
+            gathered = keep.tile([P, len(passes), (e1 - e0) * C], U32, name=tag, align_bytes=64)
+            for place, s in enumerate(passes):
+                window = x_tok[:, s * T : window_end(s)].bitcast(U32)
+                nc.vector.tensor_copy(gathered[:, place, :], window.indirect(slots(e0 * C, e1 * C)))
                 for e in range(e0, e1):
-                    slot_words[e, s] = t_[:, s - s0, (e - e0) * C : (e - e0 + 1) * C]
+                    slot_words[e, s] = gathered[:, place, (e - e0) * C : (e - e0 + 1) * C]
 
         for s in range(PASSES - 1):
-            gather_words(0, 2, s, 1, f"slot_words{s}")
+            gather_words(0, 2, [s], lambda s: (s + 1) * T, f"slot_words{s}")
             if s == 0:
-                gather_scales(0, "slot_plane0")
-                gather_scales(1, "slot_plane1")
+                gather_scales(0)
+                gather_scales(1)
         for e in range(2):
-            gather_words(e, e + 1, PASSES - 1, 1, f"last_words{e}")
+            gather_words(e, e + 1, [PASSES - 1], lambda s: (s + 1) * T, f"last_words{e}")
 
-        gate_turn = banks.tile([P, P], F32, name="bank7")
-        nc.tensor.transpose(gate_turn[:], gate_rows[:], ident[:])
+        gate_turned = banks.tile([P, P], F32, name=f"bank{BANKS - 1}")
+        nc.tensor.transpose(gate_turned[:], gate_rows[:], ident[:])
         gate_cols = keep.tile([P, E * C // P], F32, name="gate_cols")
-        nc.scalar.copy(gate_cols[:], gate_turn[:, 0 : E * C // P])
+        nc.scalar.copy(gate_cols[:], gate_turned[:, 0 : E * C // P])
 
         by_slot = [keep.tile([P, 2, HALF], F32, name=f"by_slot{half}") for half in range(2)]
         by_token = [keep.tile([P, T], F32, name=f"by_token{u}") for u in range(2)]
 
-        acc, pos, pairs = {}, {}, {}
+        acc, rectified, pairs = {}, {}, {}
 
         def multiply(e, tiles, passes):
             half, c0 = divmod(e * C, HALF)
@@ -134,75 +135,61 @@ def tile_moe_sdn_lin_relu_kernel(tc, x_words, x_scales, w1_words, w1_scales, w2_
                     )
 
         def rectify(e, j):
-            pos[e, j] = ring.tile([P, 2, P, 2], F32, name="pos")
-            nc.scalar.activation(pos[e, j][:], acc[e, j][:].rearrange("s (p u d) -> s u p d", u=2, d=2), ACT.Relu)
+            rectified[e, j] = ring.tile([P, 2, P, 2], F32, name="rectified")
+            nc.scalar.activation(rectified[e, j][:], acc[e, j][:].rearrange("s (p u d) -> s u p d", u=2, d=2), ACT.Relu)
 
         def weigh(e, j):
             gated = ring.tile([P, H], BF16, name="gated")
-            nc.scalar.activation(gated[:], pos[e, j][:].rearrange("s u p d -> s (u p d)"), ACT.Copy, scale=gate_cols[:, 2 * e + j : 2 * e + j + 1])
+            tile_no = 2 * e + j
+            nc.scalar.activation(gated[:], rectified[e, j][:].rearrange("s u p d -> s (u p d)"), ACT.Copy, scale=gate_cols[:, tile_no : tile_no + 1])
             pairs[e, j] = gated[:].bitcast(F32)
 
         def turn(e):
             half, c0 = divmod(e * C, HALF)
-            turned = banks.tile([P, 2, C], F32, name=f"bank{(2,4,6,0)[e]}")
+            turned = banks.tile([P, 2, C], F32, name=f"bank{2 * (e + 1) % BANKS}")
             for j in range(2):
                 for u in range(2):
                     nc.tensor.transpose(turned[:, u, j * P : (j + 1) * P], pairs[e, j][:, u * P : (u + 1) * P], ident[:])
             nc.scalar.copy(by_slot[half][:, :, c0 : c0 + C], turned[:])
 
-        gather_words(2,4,0,4,"late_words")
-        multiply(0,(0,1),range(4))
-        rectify(0,0)
-        rectify(0,1)
-        weigh(0,0)
-        weigh(0,1)
-        multiply(1,(0,1),(0,1))
-        multiply(1,(0,),(2,3))
-        rectify(1,0)
-        turn(0)
-        multiply(1,(1,),(2,3))
-        weigh(1,0)
-        rectify(1,1)
-        weigh(1,1)
-        multiply(2,(0,),range(4))
-        rectify(2,0)
-        turn(1)
-        multiply(2,(1,),range(4))
-        weigh(2,0)
-        rectify(2,1)
-        weigh(2,1)
-        multiply(3,(0,),range(4))
-        rectify(3,0)
-        turn(2)
-        multiply(3,(1,),range(4))
-        weigh(3,0)
-        rectify(3,1)
-        weigh(3,1)
-        turn(3)
+        gather_words(2, E, range(PASSES), lambda s: PASSES * T, "late_words")
+
+        multiply(0, (0, 1), range(PASSES))
+        for step in (rectify, weigh):
+            for j in range(2):
+                step(0, j)
+        for e in range(1, E):
+            if e == 1:
+                multiply(e, (0, 1), range(2))
+            left = range(2 if e == 1 else 0, PASSES)
+            multiply(e, (0,), left)
+            rectify(e, 0)
+            turn(e - 1)
+            multiply(e, (1,), left)
+            weigh(e, 0)
+            rectify(e, 1)
+            weigh(e, 1)
+        turn(E - 1)
 
         def scatter(u, half, c0, c1):
-            cols = offsets[:, (half * HALF + c0) // 16 : (half * HALF + c1) // 16]
-            nc.vector.tensor_copy(by_token[u][:].indirect(cols), by_slot[half][:, u, c0:c1])
+            nc.vector.tensor_copy(by_token[u][:].indirect(slots(half * HALF + c0, half * HALF + c1)), by_slot[half][:, u, c0:c1])
 
-        grouped = [keep.tile([P, width, 2], F32, name=f"grouped{n}", align_bytes=64) for n, (t0, width, per_bank) in enumerate(CHUNKS)]
+        grouped = [keep.tile([P, width, 2], F32, name=f"grouped{n}", align_bytes=64) for n, (t0, width, per_bank) in enumerate(RANGES)]
         for c0 in (0, C):
             for u in range(2):
                 scatter(u, 0, c0, c0 + C)
         scatter(0, 1, 0, C)
         scatter(1, 1, 0, P)
         scatter(0, 1, C, HALF)
-        staged = {n: keep.tile([P, 2, CHUNKS[n][1]], F32, name=f"staged{n}") for n in (2, 3)}
-        for n, (t0, width, per_bank) in enumerate(CHUNKS):
+        staged = {n: keep.tile([P, 2, RANGES[n][1]], F32, name=f"staged{n}") for n in range(DIRECT, len(RANGES))}
+        for n, (t0, width, per_bank) in enumerate(RANGES):
             nc.scalar.copy(staged[n][:, 0, :] if n in staged else grouped[n][:, :, 0], by_token[0][:, t0 : t0 + width])
-        warm = banks.tile([P, H], F32, name="bank0")
-        nc.tensor.transpose(warm[:, 0:P], by_token[0][:, 0:P], ident[:])
-        for s in range(5):
-            nc.tensor.matmul_mx(out=warm[:], lhsT=slot_words[0, 0][:, 0:P].bitcast(FP8X4), lhsT_scale=slot_plane[0][:, 0:P], rhs=w1[0, 0].bitcast(FP8X4), rhs_scale=w1_plane[0][:], start=True, stop=True)
         scatter(1, 1, P, HALF)
+
         codes, scales = {}, {}
 
         def interleave(n):
-            t0, width, per_bank = CHUNKS[n]
+            t0, width, per_bank = RANGES[n]
             if n in staged:
                 nc.scalar.copy(staged[n][:, 1, :], by_token[1][:, t0 : t0 + width])
                 nc.vector.tensor_copy(grouped[n][:], staged[n][:].rearrange("p u t -> p t u"))
@@ -210,27 +197,21 @@ def tile_moe_sdn_lin_relu_kernel(tc, x_words, x_scales, w1_words, w1_scales, w2_
                 nc.vector.tensor_copy(grouped[n][:, :, 1], by_token[1][:, t0 : t0 + width])
 
         def quantise(n):
-            width = CHUNKS[n][1]
-            c_ = keep.tile([P, width], U32, name=f"codes{n}", align_bytes=64)
-            s_ = keep.tile([P, width], U8, name=f"scales{n}", align_bytes=64)
-            nc.vector.quantize_mx(out=c_[:].bitcast(FP8X4), scales=s_[:], in_=grouped[n][:].rearrange("p t u -> p (t u)").bitcast(BF16))
-            codes[n] = c_
-            scales[n] = s_
+            width = RANGES[n][1]
+            codes[n] = keep.tile([P, width], U32, name=f"codes{n}", align_bytes=64)
+            scales[n] = keep.tile([P, width], U8, name=f"scales{n}", align_bytes=64)
+            nc.vector.quantize_mx(out=codes[n][:].bitcast(FP8X4), scales=scales[n][:], in_=grouped[n][:].rearrange("p t u -> p (t u)").bitcast(BF16))
 
-        interleave(0)
-        interleave(1)
-        quantise(0)
-        quantise(1)
-        interleave(2)
-        interleave(3)
-        quantise(2)
-        quantise(3)
+        for n0 in range(0, len(RANGES), 2):
+            for step in (interleave, quantise):
+                for n in (n0, n0 + 1):
+                    step(n)
 
-        rows = out.rearrange("(m p) t -> p m t", p=P)
-        count = 0
-        for n, (t0, width, per_bank) in enumerate(CHUNKS):
+        out_rows = out.rearrange("(m p) t -> p m t", p=P)
+        result_no = 0
+        for n, (t0, width, per_bank) in enumerate(RANGES):
             for m0 in range(0, N // P, per_bank):
-                bank = banks.tile([P, H], F32, name=f"bank{(count + 1) % 8}")
+                bank = banks.tile([P, H], F32, name=f"bank{(result_no + 1) % BANKS}")
                 for m in range(m0, m0 + per_bank):
                     nc.tensor.matmul_mx(
                         out=bank[:, (m - m0) * width : (m - m0 + 1) * width],
@@ -241,10 +222,10 @@ def tile_moe_sdn_lin_relu_kernel(tc, x_words, x_scales, w1_words, w1_scales, w2_
                         start=True,
                         stop=True,
                     )
-                res = keep.tile([P, per_bank * width], F32, name=f"res{count}")
-                if count in (4, 6, 8):
-                    nc.vector.tensor_copy(res[:], bank[:, 0 : per_bank * width])
+                result = keep.tile([P, per_bank * width], F32, name=f"res{result_no}")
+                if result_no >= VECTOR_FROM and (result_no - VECTOR_FROM) % 2 == 0:
+                    nc.vector.tensor_copy(result[:], bank[:, 0 : per_bank * width])
                 else:
-                    nc.scalar.copy(res[:], bank[:, 0 : per_bank * width])
-                nc.sync.dma_start(rows[:, m0 : m0 + per_bank, t0 : t0 + width], res[:].rearrange("p (m t) -> p m t", m=per_bank))
-                count += 1
+                    nc.scalar.copy(result[:], bank[:, 0 : per_bank * width])
+                nc.sync.dma_start(out_rows[:, m0 : m0 + per_bank, t0 : t0 + width], result[:].rearrange("p (m t) -> p m t", m=per_bank))
+                result_no += 1

@@ -18,13 +18,14 @@ ACT = mybir.ActivationFunctionType
 
 P = 128
 PASSES = K // 512
-HALF = E * C // 2
+TILES = E * C // P
 BANKS = 8
 PER_COLUMN = 16
 QUADRANT = 32
 RANGES = [(0, 128, 2), (128, 128, 4), (256, 256, 2), (512, 512, 1)]
 DIRECT = 2
 VECTOR_FROM = 4
+OVERLAP = 32
 
 
 def tile_moe_sdn_lin_relu_kernel(tc, x_words, x_scales, w1_words, w1_scales, w2_words, w2_scales, gate, offs, out):
@@ -35,6 +36,13 @@ def tile_moe_sdn_lin_relu_kernel(tc, x_words, x_scales, w1_words, w1_scales, w2_
         banks = ctx.enter_context(tc.psum_pool(name="banks", bufs=1))
 
         offsets = keep.tile([P, E * C // PER_COLUMN], U16, name="offsets")
+        x_tok = keep.tile([P, PASSES * T], I32, name="x_tok", align_bytes=64)
+        w1 = {}
+
+        def load_tokens(s):
+            nc.sync.dma_start(x_tok[:, s * T : (s + 1) * T], x_words[s].rearrange("p t d -> p (t d)").bitcast(I32))
+
+        load_tokens(0)
         nc.sync.dma_start(offsets[:], offs)
 
         x_plane = keep.tile([P, T], U8, name="x_plane", align_bytes=64)
@@ -44,19 +52,15 @@ def tile_moe_sdn_lin_relu_kernel(tc, x_words, x_scales, w1_words, w1_scales, w2_
         for e in range(E):
             nc.vector.memset(w1_plane[e][:].bitcast(I32), 0)
         nc.vector.memset(w2_plane[:].bitcast(I32), 0)
+        gate_rows = keep.tile([P, P], F32, name="gate_rows")
+        nc.vector.memset(gate_rows[:], 0.0)
         ident = keep.tile([P, P], F32, name="ident")
         make_identity(nc, ident[:])
 
-        x_tok = keep.tile([P, PASSES * T], I32, name="x_tok", align_bytes=64)
-        w1 = {}
-
-        def load_tokens(s):
-            nc.sync.dma_start(x_tok[:, s * T : (s + 1) * T], x_words[s].rearrange("p t d -> p (t d)").bitcast(I32))
-
-        def load_plane(plane, scale_rows):
+        def load_plane(queue, plane, scale_rows):
             live = 4 * scale_rows.shape[0]
             for q in range(4):
-                nc.sync.dma_start(plane[QUADRANT * q : QUADRANT * q + live, :].bitcast(I32), scale_rows[:, 4 * q : 4 * q + 4, :].bitcast(I32))
+                queue.dma_start(plane[QUADRANT * q : QUADRANT * q + live, :].bitcast(I32), scale_rows[:, 4 * q : 4 * q + 4, :].bitcast(I32))
 
         def load_w1(e, s0):
             two = keep.tile([P, 2, H], I32, name=f"w1_{e}_{s0}", align_bytes=64)
@@ -64,135 +68,123 @@ def tile_moe_sdn_lin_relu_kernel(tc, x_words, x_scales, w1_words, w1_scales, w2_
             for s in range(2):
                 w1[e, s0 + s] = two[:, s, :]
 
-        gate_rows = keep.tile([P, P], F32, name="gate_rows")
-        nc.gpsimd.memset(gate_rows[:], 0.0)
-
-        load_tokens(0)
-        load_plane(x_plane, x_scales)
-        nc.sync.dma_start(gate_rows[0 : E * C // P, :], gate[0].rearrange("(c p) -> c p", p=P))
+        side = nc.gpsimd
+        load_plane(nc.sync, x_plane, x_scales)
+        nc.sync.dma_start(gate_rows[0:TILES, :], gate[0].rearrange("(c p) -> c p", p=P))
         load_tokens(1)
-        for e in range(E):
+        load_w1(0, 0)
+        load_plane(nc.sync, w1_plane[0], w1_scales[0])
+        load_tokens(2)
+        load_tokens(3)
+        load_plane(nc.sync, w1_plane[1], w1_scales[1])
+        for e in range(2, E):
+            load_plane(side, w1_plane[e], w1_scales[e])
+        load_w1(0, 2)
+        for e in range(1, E):
             load_w1(e, 0)
-            load_plane(w1_plane[e], w1_scales[e])
-            if e == 0:
-                load_tokens(2)
-                load_tokens(3)
             load_w1(e, 2)
         w2 = keep.tile([P, 2 * N], U8, name="w2", align_bytes=64)
         nc.sync.dma_start(w2[:].bitcast(I32), w2_words[0].bitcast(I32))
         for q in range(4):
-            nc.sync.dma_start(w2_plane[QUADRANT * q : QUADRANT * q + 4, :].bitcast(I32), w2_scales[0, 4 * q : 4 * q + 4, :].bitcast(I32))
+            side.dma_start(w2_plane[QUADRANT * q : QUADRANT * q + 4, :].bitcast(I32), w2_scales[0, 4 * q : 4 * q + 4, :].bitcast(I32))
 
         def slots(first, last):
             return offsets[:, first // PER_COLUMN : last // PER_COLUMN]
 
         slot_words, slot_plane = {}, {}
 
-        def gather_scales(half):
-            slot_plane[half] = keep.tile([P, HALF], U8, name=f"slot_plane{half}", align_bytes=64)
-            nc.vector.tensor_copy(slot_plane[half][:], x_plane[:].indirect(slots(half * HALF, (half + 1) * HALF)))
+        def gather_scales(e0, e1):
+            gathered = keep.tile([P, (e1 - e0) * C], U8, name=f"slot_plane{e0}", align_bytes=64)
+            nc.vector.tensor_copy(gathered[:], x_plane[:].indirect(slots(e0 * C, e1 * C)))
+            for e in range(e0, e1):
+                slot_plane[e] = (gathered, (e - e0) * C)
 
-        def gather_words(e0, e1, passes, window_end, tag):
-            gathered = keep.tile([P, len(passes), (e1 - e0) * C], U32, name=tag, align_bytes=64)
-            for place, s in enumerate(passes):
-                window = x_tok[:, s * T : window_end(s)].bitcast(U32)
-                nc.vector.tensor_copy(gathered[:, place, :], window.indirect(slots(e0 * C, e1 * C)))
-                for e in range(e0, e1):
-                    slot_words[e, s] = gathered[:, place, (e - e0) * C : (e - e0 + 1) * C]
+        def gather_words(s, e0, e1, late):
+            gathered = keep.tile([P, (e1 - e0) * C], U32, name=f"slot_words{s}_{e0}", align_bytes=64)
+            end = max((s + 1) * T, (PASSES - 1) * T + OVERLAP) if late else (s + 1) * T
+            nc.vector.tensor_copy(gathered[:], x_tok[:, s * T : end].bitcast(U32).indirect(slots(e0 * C, e1 * C)))
+            for e in range(e0, e1):
+                slot_words[e, s] = gathered[:, (e - e0) * C : (e - e0 + 1) * C]
 
-        for s in range(PASSES - 1):
-            gather_words(0, 2, [s], lambda s: (s + 1) * T, f"slot_words{s}")
-            if s == 0:
-                gather_scales(0)
-                gather_scales(1)
-        for e in range(2):
-            gather_words(e, e + 1, [PASSES - 1], lambda s: (s + 1) * T, f"last_words{e}")
+        gather_words(0, 0, 2, False)
+        gather_scales(0, 2)
+        gather_words(1, 0, 2, False)
+        gather_scales(2, 4)
+        gather_words(2, 0, 3, False)
+        gather_words(3, 0, 1, False)
+        gather_words(3, 1, 2, False)
+        gather_words(0, 2, 4, True)
+        gather_words(1, 2, 4, True)
+        gather_words(3, 2, 4, True)
+        gather_words(2, 3, 4, True)
 
         gate_turned = banks.tile([P, P], F32, name=f"bank{BANKS - 1}")
         nc.tensor.transpose(gate_turned[:], gate_rows[:], ident[:])
-        gate_cols = keep.tile([P, E * C // P], F32, name="gate_cols")
-        nc.scalar.copy(gate_cols[:], gate_turned[:, 0 : E * C // P])
+        gate_cols = keep.tile([P, TILES], F32, name="gate_cols")
+        nc.scalar.copy(gate_cols[:], gate_turned[:, 0:TILES])
 
-        by_slot = [keep.tile([P, 2, HALF], F32, name=f"by_slot{half}") for half in range(2)]
-        by_token = [keep.tile([P, T], F32, name=f"by_token{u}") for u in range(2)]
+        staged_from = RANGES[DIRECT][0]
+        by_slot = keep.tile([P, 2, E * C], F32, name="by_slot")
+        by_token = [keep.tile([P, 2 * T - staged_from], F32, name="by_token0"), keep.tile([P, T], F32, name="by_token1")]
+        acc = {}
 
-        acc, rectified, pairs = {}, {}, {}
-
-        def multiply(e, tiles, passes):
-            half, c0 = divmod(e * C, HALF)
+        def multiply(t, passes):
+            e, j = divmod(t, 2)
+            plane, c0 = slot_plane[e]
             for s in passes:
-                for j in tiles:
-                    if s == 0:
-                        acc[e, j] = banks.tile([P, H], F32, name=f"bank{2 * e + j}")
-                    nc.tensor.matmul_mx(
-                        out=acc[e, j][:],
-                        lhsT=slot_words[e, s][:, j * P : (j + 1) * P].bitcast(FP8X4),
-                        lhsT_scale=slot_plane[half][4 * s :, c0 + j * P : c0 + (j + 1) * P],
-                        rhs=w1[e, s].bitcast(FP8X4),
-                        rhs_scale=w1_plane[e][4 * s :, :],
-                        start=(s == 0),
-                        stop=(s == PASSES - 1),
-                    )
+                if s == 0:
+                    acc[t] = banks.tile([P, H], F32, name=f"bank{t}")
+                nc.tensor.matmul_mx(
+                    out=acc[t][:],
+                    lhsT=slot_words[e, s][:, j * P : (j + 1) * P].bitcast(FP8X4),
+                    lhsT_scale=plane[4 * s :, c0 + j * P : c0 + (j + 1) * P],
+                    rhs=w1[e, s].bitcast(FP8X4),
+                    rhs_scale=w1_plane[e][4 * s :, :],
+                    start=(s == 0),
+                    stop=(s == PASSES - 1),
+                )
 
-        def rectify(e, j):
-            rectified[e, j] = ring.tile([P, 2, P, 2], F32, name="rectified")
-            nc.scalar.activation(rectified[e, j][:], acc[e, j][:].rearrange("s (p u d) -> s u p d", u=2, d=2), ACT.Relu)
-
-        def weigh(e, j):
+        def finish(t):
+            rectified = ring.tile([P, 2, P, 2], F32, name="rectified")
+            nc.scalar.activation(rectified[:], acc[t][:].rearrange("s (p u d) -> s u p d", u=2, d=2), ACT.Relu)
             gated = ring.tile([P, H], BF16, name="gated")
-            tile_no = 2 * e + j
-            nc.scalar.activation(gated[:], rectified[e, j][:].rearrange("s u p d -> s (u p d)"), ACT.Copy, scale=gate_cols[:, tile_no : tile_no + 1])
-            pairs[e, j] = gated[:].bitcast(F32)
+            nc.scalar.activation(gated[:], rectified[:].rearrange("s u p d -> s (u p d)"), ACT.Copy, scale=gate_cols[:, t : t + 1])
+            pairs = gated[:].bitcast(F32)
+            turned = banks.tile([P, 2, P], F32, name=f"bank{t}")
+            for u in range(2):
+                nc.tensor.transpose(turned[:, u, :], pairs[:, u * P : (u + 1) * P], ident[:])
+            nc.scalar.copy(by_slot[:, :, t * P : (t + 1) * P], turned[:])
 
-        def turn(e):
-            half, c0 = divmod(e * C, HALF)
-            turned = banks.tile([P, 2, C], F32, name=f"bank{2 * (e + 1) % BANKS}")
+        for e in range(E):
+            for s in range(2):
+                for j in range(2):
+                    multiply(2 * e + j, [s])
             for j in range(2):
-                for u in range(2):
-                    nc.tensor.transpose(turned[:, u, j * P : (j + 1) * P], pairs[e, j][:, u * P : (u + 1) * P], ident[:])
-            nc.scalar.copy(by_slot[half][:, :, c0 : c0 + C], turned[:])
+                multiply(2 * e + j, [2, 3])
+                finish(2 * e + j)
 
-        gather_words(2, E, range(PASSES), lambda s: PASSES * T, "late_words")
-
-        multiply(0, (0, 1), range(PASSES))
-        for step in (rectify, weigh):
-            for j in range(2):
-                step(0, j)
-        for e in range(1, E):
-            if e == 1:
-                multiply(e, (0, 1), range(2))
-            left = range(2 if e == 1 else 0, PASSES)
-            multiply(e, (0,), left)
-            rectify(e, 0)
-            turn(e - 1)
-            multiply(e, (1,), left)
-            weigh(e, 0)
-            rectify(e, 1)
-            weigh(e, 1)
-        turn(E - 1)
-
-        def scatter(u, half, c0, c1):
-            nc.vector.tensor_copy(by_token[u][:].indirect(slots(half * HALF + c0, half * HALF + c1)), by_slot[half][:, u, c0:c1])
+        def scatter(u, t0, t1):
+            nc.vector.tensor_copy(by_token[u][:].indirect(slots(t0 * P, t1 * P)), by_slot[:, u, t0 * P : t1 * P])
 
         grouped = [keep.tile([P, width, 2], F32, name=f"grouped{n}", align_bytes=64) for n, (t0, width, per_bank) in enumerate(RANGES)]
-        for c0 in (0, C):
-            for u in range(2):
-                scatter(u, 0, c0, c0 + C)
-        scatter(0, 1, 0, C)
-        scatter(1, 1, 0, P)
-        scatter(0, 1, C, HALF)
-        staged = {n: keep.tile([P, 2, RANGES[n][1]], F32, name=f"staged{n}") for n in range(DIRECT, len(RANGES))}
-        for n, (t0, width, per_bank) in enumerate(RANGES):
-            nc.scalar.copy(staged[n][:, 0, :] if n in staged else grouped[n][:, :, 0], by_token[0][:, t0 : t0 + width])
-        scatter(1, 1, P, HALF)
+        scatter(1, 0, 1)
+        for e in range(E):
+            scatter(0, 2 * e, 2 * e + 2)
+            if e == E - 1:
+                for n in range(DIRECT):
+                    t0, width, per_bank = RANGES[n]
+                    nc.scalar.copy(grouped[n][:, :, 0], by_token[0][:, t0 : t0 + width])
+            scatter(1, 2 * e + 1, min(2 * e + 3, TILES))
 
         codes, scales = {}, {}
+        both = by_token[0][:, staged_from:].rearrange("p (u t) -> p t u", u=2)
 
         def interleave(n):
             t0, width, per_bank = RANGES[n]
-            if n in staged:
-                nc.scalar.copy(staged[n][:, 1, :], by_token[1][:, t0 : t0 + width])
-                nc.vector.tensor_copy(grouped[n][:], staged[n][:].rearrange("p u t -> p t u"))
+            if n >= DIRECT:
+                x0 = t0 - staged_from
+                nc.scalar.copy(by_token[0][:, T + x0 : T + x0 + width], by_token[1][:, t0 : t0 + width])
+                nc.vector.tensor_copy(grouped[n][:], both[:, x0 : x0 + width, :])
             else:
                 nc.vector.tensor_copy(grouped[n][:, :, 1], by_token[1][:, t0 : t0 + width])
 
@@ -204,14 +196,14 @@ def tile_moe_sdn_lin_relu_kernel(tc, x_words, x_scales, w1_words, w1_scales, w2_
 
         for n0 in range(0, len(RANGES), 2):
             for step in (interleave, quantise):
-                for n in (n0, n0 + 1):
+                for n in range(n0, min(n0 + 2, len(RANGES))):
                     step(n)
 
         out_rows = out.rearrange("(m p) t -> p m t", p=P)
         result_no = 0
         for n, (t0, width, per_bank) in enumerate(RANGES):
             for m0 in range(0, N // P, per_bank):
-                bank = banks.tile([P, H], F32, name=f"bank{(result_no + 1) % BANKS}")
+                bank = banks.tile([P, H], F32, name=f"bank{result_no % BANKS}")
                 for m in range(m0, m0 + per_bank):
                     nc.tensor.matmul_mx(
                         out=bank[:, (m - m0) * width : (m - m0 + 1) * width],

@@ -26,13 +26,14 @@ RANGES = [(0, 128, 2), (128, 128, 4), (256, 256, 2), (512, 512, 1)]
 DIRECT = 2
 VECTOR_FROM = 4
 OVERLAP = 32
+RING = 4
 
 
 def tile_moe_sdn_lin_relu_kernel(tc, x_words, x_scales, w1_words, w1_scales, w2_words, w2_scales, gate, offs, out):
     nc = tc.nc
     with ExitStack() as ctx:
         keep = ctx.enter_context(tc.tile_pool(name="keep", bufs=1))
-        ring = ctx.enter_context(tc.tile_pool(name="ring", bufs=4))
+        ring = ctx.enter_context(tc.tile_pool(name="ring", bufs=RING))
         banks = ctx.enter_context(tc.psum_pool(name="banks", bufs=1))
 
         offsets = keep.tile([P, E * C // PER_COLUMN], U16, name="offsets")
@@ -68,7 +69,6 @@ def tile_moe_sdn_lin_relu_kernel(tc, x_words, x_scales, w1_words, w1_scales, w2_
             for s in range(2):
                 w1[e, s0 + s] = two[:, s, :]
 
-        side = nc.gpsimd
         load_plane(nc.sync, x_plane, x_scales)
         nc.sync.dma_start(gate_rows[0:TILES, :], gate[0].rearrange("(c p) -> c p", p=P))
         load_tokens(1)
@@ -76,9 +76,8 @@ def tile_moe_sdn_lin_relu_kernel(tc, x_words, x_scales, w1_words, w1_scales, w2_
         load_plane(nc.sync, w1_plane[0], w1_scales[0])
         load_tokens(2)
         load_tokens(3)
-        load_plane(nc.sync, w1_plane[1], w1_scales[1])
-        for e in range(2, E):
-            load_plane(side, w1_plane[e], w1_scales[e])
+        for e in range(1, E):
+            load_plane(nc.gpsimd, w1_plane[e], w1_scales[e])
         load_w1(0, 2)
         for e in range(1, E):
             load_w1(e, 0)
@@ -86,7 +85,7 @@ def tile_moe_sdn_lin_relu_kernel(tc, x_words, x_scales, w1_words, w1_scales, w2_
         w2 = keep.tile([P, 2 * N], U8, name="w2", align_bytes=64)
         nc.sync.dma_start(w2[:].bitcast(I32), w2_words[0].bitcast(I32))
         for q in range(4):
-            side.dma_start(w2_plane[QUADRANT * q : QUADRANT * q + 4, :].bitcast(I32), w2_scales[0, 4 * q : 4 * q + 4, :].bitcast(I32))
+            nc.sync.dma_start(w2_plane[QUADRANT * q : QUADRANT * q + 4, :].bitcast(I32), w2_scales[0, 4 * q : 4 * q + 4, :].bitcast(I32))
 
         def slots(first, last):
             return offsets[:, first // PER_COLUMN : last // PER_COLUMN]
@@ -106,17 +105,16 @@ def tile_moe_sdn_lin_relu_kernel(tc, x_words, x_scales, w1_words, w1_scales, w2_
             for e in range(e0, e1):
                 slot_words[e, s] = gathered[:, (e - e0) * C : (e - e0 + 1) * C]
 
-        gather_words(0, 0, 2, False)
+        gather_words(0, 0, 2, late=False)
         gather_scales(0, 2)
-        gather_words(1, 0, 2, False)
-        gather_scales(2, 4)
-        gather_words(2, 0, 3, False)
-        gather_words(3, 0, 1, False)
-        gather_words(3, 1, 2, False)
-        gather_words(0, 2, 4, True)
-        gather_words(1, 2, 4, True)
-        gather_words(3, 2, 4, True)
-        gather_words(2, 3, 4, True)
+        gather_words(1, 0, 2, late=False)
+        gather_scales(2, E)
+        gather_words(2, 0, 3, late=False)
+        for e in range(2):
+            gather_words(3, e, e + 1, late=False)
+        for s in (0, 1, 3):
+            gather_words(s, 2, E, late=True)
+        gather_words(2, 3, E, late=True)
 
         gate_turned = banks.tile([P, P], F32, name=f"bank{BANKS - 1}")
         nc.tensor.transpose(gate_turned[:], gate_rows[:], ident[:])
@@ -128,14 +126,14 @@ def tile_moe_sdn_lin_relu_kernel(tc, x_words, x_scales, w1_words, w1_scales, w2_
         by_token = [keep.tile([P, 2 * T - staged_from], F32, name="by_token0"), keep.tile([P, T], F32, name="by_token1")]
         acc = {}
 
-        def multiply(t, passes):
-            e, j = divmod(t, 2)
+        def multiply(tile_no, passes):
+            e, j = divmod(tile_no, 2)
             plane, c0 = slot_plane[e]
             for s in passes:
                 if s == 0:
-                    acc[t] = banks.tile([P, H], F32, name=f"bank{t}")
+                    acc[tile_no] = banks.tile([P, H], F32, name=f"bank{tile_no}")
                 nc.tensor.matmul_mx(
-                    out=acc[t][:],
+                    out=acc[tile_no][:],
                     lhsT=slot_words[e, s][:, j * P : (j + 1) * P].bitcast(FP8X4),
                     lhsT_scale=plane[4 * s :, c0 + j * P : c0 + (j + 1) * P],
                     rhs=w1[e, s].bitcast(FP8X4),
@@ -144,16 +142,16 @@ def tile_moe_sdn_lin_relu_kernel(tc, x_words, x_scales, w1_words, w1_scales, w2_
                     stop=(s == PASSES - 1),
                 )
 
-        def finish(t):
+        def finish(tile_no):
             rectified = ring.tile([P, 2, P, 2], F32, name="rectified")
-            nc.scalar.activation(rectified[:], acc[t][:].rearrange("s (p u d) -> s u p d", u=2, d=2), ACT.Relu)
+            nc.scalar.activation(rectified[:], acc[tile_no][:].rearrange("s (p u d) -> s u p d", u=2, d=2), ACT.Relu)
             gated = ring.tile([P, H], BF16, name="gated")
-            nc.scalar.activation(gated[:], rectified[:].rearrange("s u p d -> s (u p d)"), ACT.Copy, scale=gate_cols[:, t : t + 1])
+            nc.scalar.activation(gated[:], rectified[:].rearrange("s u p d -> s (u p d)"), ACT.Copy, scale=gate_cols[:, tile_no : tile_no + 1])
             pairs = gated[:].bitcast(F32)
-            turned = banks.tile([P, 2, P], F32, name=f"bank{t}")
+            turned = banks.tile([P, 2, P], F32, name=f"bank{tile_no}")
             for u in range(2):
                 nc.tensor.transpose(turned[:, u, :], pairs[:, u * P : (u + 1) * P], ident[:])
-            nc.scalar.copy(by_slot[:, :, t * P : (t + 1) * P], turned[:])
+            nc.scalar.copy(by_slot[:, :, tile_no * P : (tile_no + 1) * P], turned[:])
 
         for e in range(E):
             for s in range(2):
@@ -163,8 +161,8 @@ def tile_moe_sdn_lin_relu_kernel(tc, x_words, x_scales, w1_words, w1_scales, w2_
                 multiply(2 * e + j, [2, 3])
                 finish(2 * e + j)
 
-        def scatter(u, t0, t1):
-            nc.vector.tensor_copy(by_token[u][:].indirect(slots(t0 * P, t1 * P)), by_slot[:, u, t0 * P : t1 * P])
+        def scatter(u, first_tile, last_tile):
+            nc.vector.tensor_copy(by_token[u][:].indirect(slots(first_tile * P, last_tile * P)), by_slot[:, u, first_tile * P : last_tile * P])
 
         grouped = [keep.tile([P, width, 2], F32, name=f"grouped{n}", align_bytes=64) for n, (t0, width, per_bank) in enumerate(RANGES)]
         scatter(1, 0, 1)
@@ -182,9 +180,9 @@ def tile_moe_sdn_lin_relu_kernel(tc, x_words, x_scales, w1_words, w1_scales, w2_
         def interleave(n):
             t0, width, per_bank = RANGES[n]
             if n >= DIRECT:
-                x0 = t0 - staged_from
-                nc.scalar.copy(by_token[0][:, T + x0 : T + x0 + width], by_token[1][:, t0 : t0 + width])
-                nc.vector.tensor_copy(grouped[n][:], both[:, x0 : x0 + width, :])
+                place = t0 - staged_from
+                nc.scalar.copy(by_token[0][:, T + place : T + place + width], by_token[1][:, t0 : t0 + width])
+                nc.vector.tensor_copy(grouped[n][:], both[:, place : place + width, :])
             else:
                 nc.vector.tensor_copy(grouped[n][:, :, 1], by_token[1][:, t0 : t0 + width])
 
@@ -196,7 +194,7 @@ def tile_moe_sdn_lin_relu_kernel(tc, x_words, x_scales, w1_words, w1_scales, w2_
 
         for n0 in range(0, len(RANGES), 2):
             for step in (interleave, quantise):
-                for n in range(n0, min(n0 + 2, len(RANGES))):
+                for n in (n0, n0 + 1):
                     step(n)
 
         out_rows = out.rearrange("(m p) t -> p m t", p=P)

@@ -109,12 +109,12 @@ def tile_moe_sdn_lin_relu_kernel(tc, x_words, x_scales, w1_words, w1_scales, w2_
         gather_scales(0, 2)
         gather_words(1, 0, 2, late=False)
         gather_scales(2, E)
-        gather_words(2, 0, 3, late=False)
-        for e in range(2):
-            gather_words(3, e, e + 1, late=False)
-        for s in (0, 1, 3):
+        gather_words(2, 0, 2, late=False)
+        gather_words(3, 0, 1, late=False)
+        gather_words(3, 1, 3, late=False)
+        for s in range(PASSES - 1):
             gather_words(s, 2, E, late=True)
-        gather_words(2, 3, E, late=True)
+        gather_words(3, 3, E, late=True)
 
         gate_turned = banks.tile([P, P], F32, name=f"bank{BANKS - 1}")
         nc.tensor.transpose(gate_turned[:], gate_rows[:], ident[:])

@@ -24,7 +24,7 @@ PER_COLUMN = 16
 QUADRANT = 32
 RANGES = [(0, 128, 2), (128, 128, 4), (256, 256, 2), (512, 512, 1)]
 DIRECT = 2
-VECTOR_FROM = 4
+VECTOR_FROM = 3
 OVERLAP = 32
 RING = 4
 
@@ -182,7 +182,6 @@ def tile_moe_sdn_lin_relu_kernel(tc, x_words, x_scales, w1_words, w1_scales, w2_
             if n >= DIRECT:
                 place = t0 - staged_from
                 nc.scalar.copy(by_token[0][:, T + place : T + place + width], by_token[1][:, t0 : t0 + width])
-                nc.vector.tensor_copy(grouped[n][:], both[:, place : place + width, :])
             else:
                 nc.vector.tensor_copy(grouped[n][:, :, 1], by_token[1][:, t0 : t0 + width])
 
@@ -192,10 +191,15 @@ def tile_moe_sdn_lin_relu_kernel(tc, x_words, x_scales, w1_words, w1_scales, w2_
             scales[n] = keep.tile([P, width], U8, name=f"scales{n}", align_bytes=64)
             nc.vector.quantize_mx(out=codes[n][:].bitcast(FP8X4), scales=scales[n][:], in_=grouped[n][:].rearrange("p t u -> p (t u)").bitcast(BF16))
 
-        for n0 in range(0, len(RANGES), 2):
-            for step in (interleave, quantise):
-                for n in (n0, n0 + 1):
-                    step(n)
+        for n in range(len(RANGES)):
+            interleave(n)
+        for n in range(DIRECT):
+            quantise(n)
+        for n, copy in ((2, nc.scalar.copy), (3, nc.vector.tensor_copy)):
+            t0, width, per_bank = RANGES[n]
+            copy(grouped[n][:], both[:, t0 - staged_from : t0 - staged_from + width, :])
+        for n in range(DIRECT, len(RANGES)):
+            quantise(n)
 
         out_rows = out.rearrange("(m p) t -> p m t", p=P)
         result_no = 0

@@ -26,6 +26,7 @@ RANGES = [(0, 128, 2), (128, 128, 4), (256, 256, 2), (512, 512, 1)]
 DIRECT = 2
 VECTOR_FROM = 3
 OVERLAP = 32
+WARM_UP = 4
 RING = 4
 
 
@@ -114,7 +115,7 @@ def tile_moe_sdn_lin_relu_kernel(tc, x_words, x_scales, w1_words, w1_scales, w2_
         gather_words(3, 1, 3, late=False)
         for s in range(PASSES - 1):
             gather_words(s, 2, E, late=True)
-        gather_words(3, 3, E, late=True)
+        gather_words(3, 3, E, late=False)
 
         gate_turned = banks.tile([P, P], F32, name=f"bank{BANKS - 1}")
         nc.tensor.transpose(gate_turned[:], gate_rows[:], ident[:])
@@ -164,6 +165,20 @@ def tile_moe_sdn_lin_relu_kernel(tc, x_words, x_scales, w1_words, w1_scales, w2_
         def scatter(u, first_tile, last_tile):
             nc.vector.tensor_copy(by_token[u][:].indirect(slots(first_tile * P, last_tile * P)), by_slot[:, u, first_tile * P : last_tile * P])
 
+        def warm_up():
+            idle = banks.tile([P, H], F32, name=f"bank{TILES - 1}")
+            nc.tensor.transpose(idle[:, 0:P], by_token[1][:, 0:P], ident[:])
+            for repeat in range(WARM_UP):
+                nc.tensor.matmul_mx(
+                    out=idle[:],
+                    lhsT=slot_words[E - 1, 0][:, 0:P].bitcast(FP8X4),
+                    lhsT_scale=slot_plane[E - 1][0][:, 0:P],
+                    rhs=w1[E - 1, 0].bitcast(FP8X4),
+                    rhs_scale=w1_plane[E - 1][:],
+                    start=True,
+                    stop=True,
+                )
+
         grouped = [keep.tile([P, width, 2], F32, name=f"grouped{n}", align_bytes=64) for n, (t0, width, per_bank) in enumerate(RANGES)]
         scatter(1, 0, 1)
         for e in range(E):
@@ -173,17 +188,23 @@ def tile_moe_sdn_lin_relu_kernel(tc, x_words, x_scales, w1_words, w1_scales, w2_
                     t0, width, per_bank = RANGES[n]
                     nc.scalar.copy(grouped[n][:, :, 0], by_token[0][:, t0 : t0 + width])
             scatter(1, 2 * e + 1, min(2 * e + 3, TILES))
+            if e == E - 2:
+                warm_up()
 
         codes, scales = {}, {}
         both = by_token[0][:, staged_from:].rearrange("p (u t) -> p t u", u=2)
 
-        def interleave(n):
+        def place_strand(n):
             t0, width, per_bank = RANGES[n]
             if n >= DIRECT:
                 place = t0 - staged_from
                 nc.scalar.copy(by_token[0][:, T + place : T + place + width], by_token[1][:, t0 : t0 + width])
             else:
                 nc.vector.tensor_copy(grouped[n][:, :, 1], by_token[1][:, t0 : t0 + width])
+
+        def interleave(copy, n):
+            t0, width, per_bank = RANGES[n]
+            copy(grouped[n][:], both[:, t0 - staged_from : t0 - staged_from + width, :])
 
         def quantise(n):
             width = RANGES[n][1]
@@ -192,12 +213,11 @@ def tile_moe_sdn_lin_relu_kernel(tc, x_words, x_scales, w1_words, w1_scales, w2_
             nc.vector.quantize_mx(out=codes[n][:].bitcast(FP8X4), scales=scales[n][:], in_=grouped[n][:].rearrange("p t u -> p (t u)").bitcast(BF16))
 
         for n in range(len(RANGES)):
-            interleave(n)
+            place_strand(n)
         for n in range(DIRECT):
             quantise(n)
-        for n, copy in ((2, nc.scalar.copy), (3, nc.vector.tensor_copy)):
-            t0, width, per_bank = RANGES[n]
-            copy(grouped[n][:], both[:, t0 - staged_from : t0 - staged_from + width, :])
+        interleave(nc.scalar.copy, DIRECT)
+        interleave(nc.vector.tensor_copy, DIRECT + 1)
         for n in range(DIRECT, len(RANGES)):
             quantise(n)
 

@@ -25,6 +25,7 @@ QUADRANT = 32
 RANGES = [(0, 128, 2), (128, 128, 4), (256, 256, 2), (512, 512, 1)]
 DIRECT = 2
 VECTOR_FROM = 3
+PLACE = (2, 0, 1, 3)
 OVERLAP = 32
 WARM_UP = 4
 RING = 4
@@ -42,7 +43,7 @@ def tile_moe_sdn_lin_relu_kernel(tc, x_words, x_scales, w1_words, w1_scales, w2_
         w1 = {}
 
         def load_tokens(s):
-            nc.sync.dma_start(x_tok[:, s * T : (s + 1) * T], x_words[s].rearrange("p t d -> p (t d)").bitcast(I32))
+            nc.sync.dma_start(x_tok[:, PLACE[s] * T : (PLACE[s] + 1) * T], x_words[s].rearrange("p t d -> p (t d)").bitcast(I32))
 
         load_tokens(0)
         nc.sync.dma_start(offsets[:], offs)
@@ -101,20 +102,21 @@ def tile_moe_sdn_lin_relu_kernel(tc, x_words, x_scales, w1_words, w1_scales, w2_
 
         def gather_words(s, e0, e1, late):
             gathered = keep.tile([P, (e1 - e0) * C], U32, name=f"slot_words{s}_{e0}", align_bytes=64)
-            end = max((s + 1) * T, (PASSES - 1) * T + OVERLAP) if late else (s + 1) * T
-            nc.vector.tensor_copy(gathered[:], x_tok[:, s * T : end].bitcast(U32).indirect(slots(e0 * C, e1 * C)))
+            end = max((PLACE[s] + 1) * T, (PASSES - 1) * T + OVERLAP) if late else (PLACE[s] + 1) * T
+            nc.vector.tensor_copy(gathered[:], x_tok[:, PLACE[s] * T : end].bitcast(U32).indirect(slots(e0 * C, e1 * C)))
             for e in range(e0, e1):
                 slot_words[e, s] = gathered[:, (e - e0) * C : (e - e0 + 1) * C]
 
-        gather_words(0, 0, 2, late=False)
+        gather_words(0, 0, 3, late=False)
         gather_scales(0, 2)
         gather_words(1, 0, 2, late=False)
         gather_scales(2, E)
         gather_words(2, 0, 2, late=False)
         gather_words(3, 0, 1, late=False)
         gather_words(3, 1, 3, late=False)
-        for s in range(PASSES - 1):
+        for s in range(1, PASSES - 1):
             gather_words(s, 2, E, late=True)
+        gather_words(0, 3, E, late=True)
         gather_words(3, 3, E, late=False)
 
         gate_turned = banks.tile([P, P], F32, name=f"bank{BANKS - 1}")

@@ -78,8 +78,9 @@ def tile_moe_sdn_lin_relu_kernel(tc, x_words, x_scales, w1_words, w1_scales, w2_
         load_plane(nc.sync, w1_plane[0], w1_scales[0])
         load_tokens(2)
         load_tokens(3)
-        for e in range(1, E):
+        for e in range(2, E):
             load_plane(nc.gpsimd, w1_plane[e], w1_scales[e])
+        load_plane(nc.sync, w1_plane[1], w1_scales[1])
         load_w1(0, 2)
         for e in range(1, E):
             load_w1(e, 0)

@@ -71,9 +71,9 @@ def tile_moe_sdn_lin_relu_kernel(tc, x_words, x_scales, w1_words, w1_scales, w2_
             for s in range(2):
                 w1[e, s0 + s] = two[:, s, :]
 
+        load_tokens(1)
         load_plane(nc.sync, x_plane, x_scales)
         nc.sync.dma_start(gate_rows[0:TILES, :], gate[0].rearrange("(c p) -> c p", p=P))
-        load_tokens(1)
         load_w1(0, 0)
         load_plane(nc.sync, w1_plane[0], w1_scales[0])
         load_tokens(2)
@@ -109,8 +109,8 @@ def tile_moe_sdn_lin_relu_kernel(tc, x_words, x_scales, w1_words, w1_scales, w2_
                 slot_words[e, s] = gathered[:, (e - e0) * C : (e - e0 + 1) * C]
 
         gather_words(0, 0, 3, late=False)
-        gather_scales(0, 2)
         gather_words(1, 0, 2, late=False)
+        gather_scales(0, 2)
         gather_scales(2, E)
         gather_words(2, 0, 2, late=False)
         gather_words(3, 0, 1, late=False)

from contextlib import ExitStack

import concourse.mybir as mybir
from concourse.masks import make_identity

K, T, E, C, H, N = 2048, 1024, 4, 256, 512, 512
FLOPS = 2 * K * H * E * C + 2 * H * N * T

F32 = mybir.dt.float32
BF16 = mybir.dt.bfloat16
I32 = mybir.dt.int32
U32 = mybir.dt.uint32
U16 = mybir.dt.uint16
U8 = mybir.dt.uint8
FP8X4 = mybir.dt.float8_e4m3fn_x4
FP4X4 = mybir.dt.float4_e2m1fn_x4
ACT = mybir.ActivationFunctionType

P = 128
PASSES = K // 512
TILES = E * C // P
BANKS = 8
PER_COLUMN = 16
QUADRANT = 32
RANGES = [(0, 128, 2), (128, 128, 4), (256, 256, 2), (512, 512, 1)]
DIRECT = 2
VECTOR_FROM = 3
PLACE = (2, 0, 1, 3)
OVERLAP = 32
WARM_UP = 4
RING = 4


def tile_moe_sdn_lin_relu_kernel(tc, x_words, x_scales, w1_words, w1_scales, w2_words, w2_scales, gate, offs, out):
    nc = tc.nc
    with ExitStack() as ctx:
        keep = ctx.enter_context(tc.tile_pool(name="keep", bufs=1))
        ring = ctx.enter_context(tc.tile_pool(name="ring", bufs=RING))
        banks = ctx.enter_context(tc.psum_pool(name="banks", bufs=1))

        offsets = keep.tile([P, E * C // PER_COLUMN], U16, name="offsets")
        x_tok = keep.tile([P, PASSES * T], I32, name="x_tok", align_bytes=64)
        w1 = {}

        def load_tokens(s):
            nc.sync.dma_start(x_tok[:, PLACE[s] * T : (PLACE[s] + 1) * T], x_words[s].rearrange("p t d -> p (t d)").bitcast(I32))

        load_tokens(0)
        nc.sync.dma_start(offsets[:], offs)

        x_plane = keep.tile([P, T], U8, name="x_plane", align_bytes=64)
        w1_plane = [keep.tile([P, H], U8, name=f"w1_plane{e}", align_bytes=64) for e in range(E)]
        w2_plane = keep.tile([P, N], U8, name="w2_plane", align_bytes=64)
        nc.gpsimd.memset(x_plane[:].bitcast(I32), 0)
        for e in range(E):
            nc.vector.memset(w1_plane[e][:].bitcast(I32), 0)
        nc.vector.memset(w2_plane[:].bitcast(I32), 0)
        gate_rows = keep.tile([P, P], F32, name="gate_rows")
        nc.vector.memset(gate_rows[:], 0.0)
        ident = keep.tile([P, P], F32, name="ident")
        make_identity(nc, ident[:])

        def load_plane(queue, plane, scale_rows):
            live = 4 * scale_rows.shape[0]
            for q in range(4):
                queue.dma_start(plane[QUADRANT * q : QUADRANT * q + live, :].bitcast(I32), scale_rows[:, 4 * q : 4 * q + 4, :].bitcast(I32))

        def load_w1(e, s0):
            two = keep.tile([P, 2, H], I32, name=f"w1_{e}_{s0}", align_bytes=64)
            nc.sync.dma_start(two[:], w1_words[e, s0 : s0 + 2].rearrange("s p i d -> p s (i d)").bitcast(I32))
            for s in range(2):
                w1[e, s0 + s] = two[:, s, :]

        load_tokens(1)
        load_plane(nc.sync, x_plane, x_scales)
        nc.sync.dma_start(gate_rows[0:TILES, :], gate[0].rearrange("(c p) -> c p", p=P))
        load_w1(0, 0)
        load_plane(nc.sync, w1_plane[0], w1_scales[0])
        load_tokens(2)
        load_tokens(3)
        for e in range(2, E):
            load_plane(nc.gpsimd, w1_plane[e], w1_scales[e])
        load_plane(nc.sync, w1_plane[1], w1_scales[1])
        load_w1(0, 2)
        for e in range(1, E):
            load_w1(e, 0)
            load_w1(e, 2)
        w2 = keep.tile([P, 2 * N], U8, name="w2", align_bytes=64)
        nc.sync.dma_start(w2[:].bitcast(I32), w2_words[0].bitcast(I32))
        for q in range(4):
            nc.sync.dma_start(w2_plane[QUADRANT * q : QUADRANT * q + 4, :].bitcast(I32), w2_scales[0, 4 * q : 4 * q + 4, :].bitcast(I32))

        def slots(first, last):
            return offsets[:, first // PER_COLUMN : last // PER_COLUMN]

        slot_words, slot_plane = {}, {}

        def gather_scales(e0, e1):
            gathered = keep.tile([P, (e1 - e0) * C], U8, name=f"slot_plane{e0}", align_bytes=64)
            nc.vector.tensor_copy(gathered[:], x_plane[:].indirect(slots(e0 * C, e1 * C)))
            for e in range(e0, e1):
                slot_plane[e] = (gathered, (e - e0) * C)

        def gather_words(s, e0, e1, late):
            gathered = keep.tile([P, (e1 - e0) * C], U32, name=f"slot_words{s}_{e0}", align_bytes=64)
            end = max((PLACE[s] + 1) * T, (PASSES - 1) * T + OVERLAP) if late else (PLACE[s] + 1) * T
            nc.vector.tensor_copy(gathered[:], x_tok[:, PLACE[s] * T : end].bitcast(U32).indirect(slots(e0 * C, e1 * C)))
            for e in range(e0, e1):
                slot_words[e, s] = gathered[:, (e - e0) * C : (e - e0 + 1) * C]

        gather_words(0, 0, 3, late=False)
        gather_words(1, 0, 2, late=False)
        gather_scales(0, 2)
        gather_scales(2, E)
        gather_words(2, 0, 2, late=False)
        gather_words(3, 0, 1, late=False)
        gather_words(3, 1, 3, late=False)
        for s in range(1, PASSES - 1):
            gather_words(s, 2, E, late=True)
        gather_words(0, 3, E, late=True)
        gather_words(3, 3, E, late=False)

        gate_turned = banks.tile([P, P], F32, name=f"bank{BANKS - 1}")
        nc.tensor.transpose(gate_turned[:], gate_rows[:], ident[:])
        gate_cols = keep.tile([P, TILES], F32, name="gate_cols")
        nc.scalar.copy(gate_cols[:], gate_turned[:, 0:TILES])

        staged_from = RANGES[DIRECT][0]
        by_slot = keep.tile([P, 2, E * C], F32, name="by_slot")
        by_token = [keep.tile([P, 2 * T - staged_from], F32, name="by_token0"), keep.tile([P, T], F32, name="by_token1")]
        acc = {}

        def multiply(tile_no, passes):
            e, j = divmod(tile_no, 2)
            plane, c0 = slot_plane[e]
            for s in passes:
                if s == 0:
                    acc[tile_no] = banks.tile([P, H], F32, name=f"bank{tile_no}")
                nc.tensor.matmul_mx(
                    out=acc[tile_no][:],
                    lhsT=slot_words[e, s][:, j * P : (j + 1) * P].bitcast(FP8X4),
                    lhsT_scale=plane[4 * s :, c0 + j * P : c0 + (j + 1) * P],
                    rhs=w1[e, s].bitcast(FP8X4),
                    rhs_scale=w1_plane[e][4 * s :, :],
                    start=(s == 0),
                    stop=(s == PASSES - 1),
                )

        def finish(tile_no):
            rectified = ring.tile([P, 2, P, 2], F32, name="rectified")
            nc.scalar.activation(rectified[:], acc[tile_no][:].rearrange("s (p u d) -> s u p d", u=2, d=2), ACT.Relu)
            gated = ring.tile([P, H], BF16, name="gated")
            nc.scalar.activation(gated[:], rectified[:].rearrange("s u p d -> s (u p d)"), ACT.Copy, scale=gate_cols[:, tile_no : tile_no + 1])
            pairs = gated[:].bitcast(F32)
            turned = banks.tile([P, 2, P], F32, name=f"bank{tile_no}")
            for u in range(2):
                nc.tensor.transpose(turned[:, u, :], pairs[:, u * P : (u + 1) * P], ident[:])
            nc.scalar.copy(by_slot[:, :, tile_no * P : (tile_no + 1) * P], turned[:])

        for e in range(E):
            for s in range(2):
                for j in range(2):
                    multiply(2 * e + j, [s])
            for j in range(2):
                multiply(2 * e + j, [2, 3])
                finish(2 * e + j)

        def scatter(u, first_tile, last_tile):
            nc.vector.tensor_copy(by_token[u][:].indirect(slots(first_tile * P, last_tile * P)), by_slot[:, u, first_tile * P : last_tile * P])

        def warm_up():
            idle = banks.tile([P, H], F32, name=f"bank{TILES - 1}")
            nc.tensor.transpose(idle[:, 0:P], by_token[1][:, 0:P], ident[:])
            for repeat in range(WARM_UP):
                nc.tensor.matmul_mx(
                    out=idle[:],
                    lhsT=slot_words[E - 1, 0][:, 0:P].bitcast(FP8X4),
                    lhsT_scale=slot_plane[E - 1][0][:, 0:P],
                    rhs=w1[E - 1, 0].bitcast(FP8X4),
                    rhs_scale=w1_plane[E - 1][:],
                    start=True,
                    stop=True,
                )

        grouped = [keep.tile([P, width, 2], F32, name=f"grouped{n}", align_bytes=64) for n, (t0, width, per_bank) in enumerate(RANGES)]
        scatter(1, 0, 1)
        for e in range(E):
            scatter(0, 2 * e, 2 * e + 2)
            if e == E - 1:
                for n in range(DIRECT):
                    t0, width, per_bank = RANGES[n]
                    nc.scalar.copy(grouped[n][:, :, 0], by_token[0][:, t0 : t0 + width])
            scatter(1, 2 * e + 1, min(2 * e + 3, TILES))
            if e == E - 2:
                warm_up()

        codes, scales = {}, {}
        both = by_token[0][:, staged_from:].rearrange("p (u t) -> p t u", u=2)

        def place_strand(n):
            t0, width, per_bank = RANGES[n]
            if n >= DIRECT:
                place = t0 - staged_from
                nc.scalar.copy(by_token[0][:, T + place : T + place + width], by_token[1][:, t0 : t0 + width])
            else:
                nc.vector.tensor_copy(grouped[n][:, :, 1], by_token[1][:, t0 : t0 + width])

        def interleave(copy, n):
            t0, width, per_bank = RANGES[n]
            copy(grouped[n][:], both[:, t0 - staged_from : t0 - staged_from + width, :])

        def quantise(n):
            width = RANGES[n][1]
            codes[n] = keep.tile([P, width], U32, name=f"codes{n}", align_bytes=64)
            scales[n] = keep.tile([P, width], U8, name=f"scales{n}", align_bytes=64)
            nc.vector.quantize_mx(out=codes[n][:].bitcast(FP8X4), scales=scales[n][:], in_=grouped[n][:].rearrange("p t u -> p (t u)").bitcast(BF16))

        for n in range(len(RANGES)):
            place_strand(n)
        for n in range(DIRECT):
            quantise(n)
        interleave(nc.scalar.copy, DIRECT)
        interleave(nc.vector.tensor_copy, DIRECT + 1)
        for n in range(DIRECT, len(RANGES)):
            quantise(n)

        out_rows = out.rearrange("(m p) t -> p m t", p=P)
        result_no = 0
        for n, (t0, width, per_bank) in enumerate(RANGES):
            for m0 in range(0, N // P, per_bank):
                bank = banks.tile([P, H], F32, name=f"bank{result_no % BANKS}")
                for m in range(m0, m0 + per_bank):
                    nc.tensor.matmul_mx(
                        out=bank[:, (m - m0) * width : (m - m0 + 1) * width],
                        lhsT=w2[:, 2 * m * P : 2 * (m + 1) * P].bitcast(FP4X4),
                        lhsT_scale=w2_plane[:, m * P : (m + 1) * P],
                        rhs=codes[n][:].bitcast(FP8X4),
                        rhs_scale=scales[n][:],
                        start=True,
                        stop=True,
                    )
                result = keep.tile([P, per_bank * width], F32, name=f"res{result_no}")
                if result_no >= VECTOR_FROM and (result_no - VECTOR_FROM) % 2 == 0:
                    nc.vector.tensor_copy(result[:], bank[:, 0 : per_bank * width])
                else:
                    nc.scalar.copy(result[:], bank[:, 0 : per_bank * width])
                nc.sync.dma_start(out_rows[:, m0 : m0 + per_bank, t0 : t0 + width], result[:].rearrange("p (m t) -> p m t", m=per_bank))
                result_no += 1
